import numpy as np
import ml_dtypes


def mxq(x, axis, fmt="e4m3"):
    dtype, down = {"e4m3": (ml_dtypes.float8_e4m3fn, 7), "e5m2": (ml_dtypes.float8_e5m2, 14)}[fmt]
    v = np.moveaxis(np.asarray(x, np.float32).astype(ml_dtypes.bfloat16).astype(np.float64), axis, -1)
    blocks = v.reshape(v.shape[:-1] + (-1, 32))
    amax = np.abs(blocks).max(-1, keepdims=True)
    byte = np.maximum(np.where(amax > 0, np.frexp(amax)[1] - 1 + 127, 0) - down, 1)
    scale = np.exp2(byte - 127.0)
    codes = (blocks / scale).astype(np.float32).astype(dtype).astype(np.float64)
    return np.moveaxis((codes * scale).reshape(v.shape), -1, axis)


WIDE = False


def mx_kscale(k):
    if not WIDE:
        return np.ones(k)
    levels = np.array([30, -30])
    if k % 512:
        return np.exp2(np.random.permutation(np.resize(levels, k // 32))).repeat(32)
    a = np.empty((k // 512, 16))
    for p in range(k // 512):
        a[p, :8] = np.random.permutation(np.resize(levels, 8))
        for g in range(8):
            far = levels[np.abs(levels - a[p, g]) >= 10]
            a[p, g + 8] = far[np.random.randint(len(far))]
    return np.exp2(a.ravel()).repeat(32)


def f64(x):
    return np.asarray(x).astype(np.float64)


def striped(idx):
    return np.tile(idx.reshape(-1, 16).T, (8, 1)).astype(np.uint16)


def unstriped(offs):
    return offs[:16].T.reshape(-1).astype(np.int64)


E2M1 = np.array([0.0, 0.5, 1.0, 1.5, 2.0, 3.0, 4.0, 6.0, -0.0, -0.5, -1.0, -1.5, -2.0, -3.0, -4.0, -6.0])


def pack_weight(w, fmt):
    k, n = w.shape
    w = f64(np.asarray(w, np.float32).astype(ml_dtypes.bfloat16)).reshape(k // 32, 32, n)
    amax = np.abs(w).max(1)
    if fmt == "e4m3":
        byte = np.frexp(amax)[1] - 1 + 127 - 7
    elif fmt == "e5m2":
        byte = np.frexp(amax)[1] - 1 + 127 - 14
    else:
        mant, ex = np.frexp(amax / 6.0)
        byte = np.where(mant > 0.5, ex, ex - 1) + 127
    byte = np.clip(np.where(amax > 0, byte, 1), 1, 254)
    scaled = (w * np.exp2(127.0 - byte)[:, None, :]).reshape(k, n).astype(np.float32)
    by_word = np.ascontiguousarray(scaled.reshape(k // 512, 128, 4, n).transpose(0, 1, 3, 2))
    if fmt == "e4m3":
        words = by_word.astype(ml_dtypes.float8_e4m3fn).view(np.uint8)
    elif fmt == "e5m2":
        words = by_word.astype(ml_dtypes.float8_e5m2).view(np.uint8)
    else:
        c = by_word.astype(ml_dtypes.float4_e2m1fn).view(np.uint8) & 0xF
        words = (c[..., 0::2] | (c[..., 1::2] << 4)).reshape(k // 512, 128, 2 * n)
    return np.ascontiguousarray(words), np.ascontiguousarray(byte.astype(np.uint8).reshape(k // 512, 16, n))


def unpack_weight(words, scales, fmt):
    g, _, n = scales.shape
    words = np.ascontiguousarray(words).reshape(g, 128, n, -1)
    if fmt == "e4m3":
        vals = words.view(ml_dtypes.float8_e4m3fn).astype(np.float64)
    elif fmt == "e5m2":
        vals = words.view(ml_dtypes.float8_e5m2).astype(np.float64)
    else:
        nib = np.empty((g, 128, n, 4), np.uint8)
        nib[..., 0::2] = words & 0xF
        nib[..., 1::2] = words >> 4
        vals = E2M1[nib]
    vals = vals * np.repeat(np.exp2(scales.astype(np.float64) - 127.0), 8, axis=1)[..., None]
    return vals.transpose(0, 1, 3, 2).reshape(g * 512, n)


def d_relu(v):
    return (v > 0).astype(np.float64)


K, T, E, C, H, N = 512, 1024, 2, 512, 512, 512


def by_expert(wq, xq):
    return np.concatenate([wq[e].T @ xq[:, e * C:(e + 1) * C] for e in range(E)], axis=1)


def setup_inputs():
    n = np.random.standard_normal
    v = mx_kscale(N)
    u = mx_kscale(H)
    slot_token = np.random.permutation(T)[:E * C]
    w_slot = np.random.uniform(0.2, 1.0, E * C)
    dy = pack_weight(n((N, T)) * v[:, None], "e5m2")
    w2t = pack_weight(n((N, H)) / np.sqrt(N) / v[:, None] * u, "e4m3")
    w1t = [pack_weight(m, "e4m3") for m in n((E, H, K)) / np.sqrt(H) / u[None, :, None]]
    return {
        "dy_words": dy[0],
        "dy_scales": dy[1],
        "w2t_words": w2t[0],
        "w2t_scales": w2t[1],
        "w1t_words": np.stack([m[0] for m in w1t]),
        "w1t_scales": np.stack([m[1] for m in w1t]),
        "a": (n((H, E * C))).astype(np.float32),
        "gate": (np.tile(w_slot, (128, 1))).astype(np.float32),
        "offs": striped(slot_token),
    }


def reference(dy_words, dy_scales, w2t_words, w2t_scales, w1t_words, w1t_scales, a, gate, offs):
    w2t = unpack_weight(w2t_words, w2t_scales, "e4m3")
    w1t = np.stack([unpack_weight(w1t_words[e], w1t_scales[e], "e4m3") for e in range(E)])
    idx = unstriped(offs)
    dc = w2t.T @ unpack_weight(dy_words, dy_scales, "e5m2")
    da = f64(gate[:1]) * dc[:, idx] * d_relu(f64(a))
    dx = by_expert(w1t, mxq(da, 0, "e5m2"))
    out = np.zeros((K, T))
    out[:, idx] = dx
    return out

@@ -1,0 +1,176 @@
+from contextlib import ExitStack
+
+import concourse.mybir as mybir
+
+K, T, E, C, H, N = 512, 1024, 2, 512, 512, 512
+P = 128
+PACK = 4
+FLOPS = 2 * N * H * T + 2 * H * K * E * C
+
+F32 = mybir.dt.float32
+BF16 = mybir.dt.bfloat16
+I32 = mybir.dt.int32
+U16 = mybir.dt.uint16
+U8 = mybir.dt.uint8
+E4M3 = mybir.dt.float8_e4m3fn_x4
+E5M2 = mybir.dt.float8_e5m2_x4
+ALU = mybir.AluOpType
+ACT = mybir.ActivationFunctionType
+
+
+def load_scale_rows(queue, plane, rows):
+    for r in range(4):
+        queue.dma_start(out=plane[r:P:32, :].bitcast(I32), in_=rows[r:16:4, :].bitcast(I32))
+
+
+def by_four(ap):
+    return ap.rearrange("p d (c i) -> p c d i", i=4)
+
+
+def woven_by_four(ap):
+    return ap.rearrange("p (c i d) -> p c d i", i=4, d=PACK)
+
+
+def tile_moe_sdb_relu_kernel(
+    tc, dy_words, dy_scales, w2t_words, w2t_scales, w1t_words, w1t_scales, a, gate, offs, out
+):
+    nc = tc.nc
+    with ExitStack() as ctx:
+        held = ctx.enter_context(tc.tile_pool(name="held", bufs=1))
+        psum = ctx.enter_context(tc.psum_pool(name="psum", bufs=1))
+
+        offsets = held.tile([P, E * C // 16], U16, name="offsets")
+        w2_raw = held.tile([P, H], I32, name="w2_raw", align_bytes=64)
+        w2_rows = held.tile([P, H], U8, name="w2_rows", align_bytes=64)
+        w2_zeroed = held.tile([P, H], U8, name="w2_zeroed", align_bytes=64)
+        w2_codes = held.tile([P, H], I32, name="w2_codes", align_bytes=64)
+        w2_plane = held.tile([P, H], U8, name="w2_plane", align_bytes=64)
+        dy_codes = held.tile([P, T], I32, name="dy_codes", align_bytes=64)
+        dy_plane = held.tile([P, T], U8, name="dy_plane", align_bytes=64)
+        w1_codes = held.tile([P, E, K], I32, name="w1_codes", align_bytes=64)
+        w1_plane = held.tile([P, E, K], U8, name="w1_plane", align_bytes=64)
+        gates = [held.tile([P, C], F32, name=f"gate{e}") for e in range(E)]
+        a0 = [held.tile([P, C], F32, name=f"a0{d}") for d in range(PACK)]
+        rows = held.tile([P, 10, C], F32, name="rows")
+        factor = rows[:, 0:4, :]
+        da = [rows[:, 4:8, :], rows[:, 2:6, :]]
+        a1 = rows[:, 6:10, :]
+
+        nc.vector.memset(w2_zeroed[:].bitcast(I32), 0)
+
+        load_scale_rows(nc.sync, w2_rows, w2t_scales[0])
+        nc.sync.dma_start(out=w2_raw[:], in_=w2t_words[0].rearrange("p i d -> p (i d)").bitcast(I32))
+        nc.sync.dma_start(out=dy_codes[:], in_=dy_words[0].rearrange("p t d -> p (t d)").bitcast(I32))
+        for r in range(4):
+            queue = nc.sync
+            queue.dma_start(out=dy_plane[r:P:32, :].bitcast(I32), in_=dy_scales[0][r:16:4, :].bitcast(I32))
+        a_rows = a.rearrange("(p d) s -> p d s", d=PACK)
+        nc.sync.dma_start(out=gates[0][:], in_=gate[:, 0:C])
+        nc.sync.dma_start(out=a0[0][:], in_=a_rows[:, 0, 0:C])
+        nc.sync.dma_start(out=a0[1][:], in_=a_rows[:, 1, 0:C])
+        nc.sync.dma_start(offsets[:], offs)
+        for d in range(2, PACK):
+            nc.sync.dma_start(out=a0[d][:], in_=a_rows[:, d, 0:C])
+        nc.sync.dma_start(out=gates[1][:], in_=gate[:, C : 2 * C])
+        nc.sync.dma_start(out=w1_codes[:], in_=w1t_words[:, 0].rearrange("e p k d -> p e (k d)").bitcast(I32))
+        for r in range(4):
+            nc.sync.dma_start(
+                out=w1_plane[r:P:32, :, :].bitcast(I32),
+                in_=w1t_scales[:, 0, r:16:4, :].rearrange("e q k -> q e k").bitcast(I32),
+            )
+
+        for q in range(4):
+            live = slice(32 * q, 32 * q + 4)
+            nc.vector.tensor_copy(out=w2_zeroed[live, :].bitcast(I32), in_=w2_rows[live, :].bitcast(I32))
+        nc.vector.tensor_copy(
+            out=w2_codes[:].rearrange("p (d m) -> p d m", d=PACK), in_=w2_raw[:].rearrange("p (m d) -> p d m", d=PACK)
+        )
+        nc.vector.tensor_copy(
+            out=w2_plane[:].rearrange("p (d m) -> p d m", d=PACK), in_=w2_zeroed[:].rearrange("p (m d) -> p d m", d=PACK)
+        )
+
+        banks = [psum.tile([P, C], F32, name=f"bank{b}") for b in range(8)]
+        dc = [held.tile([P, T], F32, name=f"dc{d}") for d in range(PACK)]
+        for d in range(PACK):
+            cols = slice(d * P, (d + 1) * P)
+            for h in range(2):
+                toks = slice(h * C, (h + 1) * C)
+                bank = banks[2 * d + h]
+                nc.tensor.matmul_mx(
+                    out=bank[:], lhsT=w2_codes[:, cols].bitcast(E4M3), lhsT_scale=w2_plane[:, cols],
+                    rhs=dy_codes[:, toks].bitcast(E5M2), rhs_scale=dy_plane[:, toks], start=True, stop=True,
+                )
+                nc.scalar.copy(out=dc[d][:, toks], in_=bank[:])
+
+        woven = [held.tile([P, C * PACK], BF16, name=f"woven{e}", align_bytes=64) for e in range(E)]
+        da_codes = [held.tile([P, C], I32, name=f"da_codes{e}", align_bytes=64) for e in range(E)]
+        da_plane = [held.tile([P, C], U8, name=f"da_plane{e}", align_bytes=64) for e in range(E)]
+        window = [held.tile([P, T], F32, name=f"window{b}") for b in range(4)]
+        dx = {}
+
+        def expert_list(e):
+            return offsets[:, e * C // 16 : (e + 1) * C // 16]
+
+        def gather(e, d, other):
+            nc.vector.tensor_tensor(da[e][:, d, :], dc[d][:].indirect(expert_list(e)), other, ALU.mult)
+
+        def weave(e):
+            nc.scalar.copy(out=woven_by_four(woven[e][:]), in_=by_four(da[e]))
+
+        def quantize(e, values):
+            nc.vector.quantize_mx(out=da_codes[e][:].bitcast(E5M2), scales=da_plane[e][:], in_=values)
+
+        def product(e, b, tag=""):
+            cols = slice(b * P, (b + 1) * P)
+            bank = banks[4 * e + b]
+            nc.tensor.matmul_mx(
+                out=bank[:], lhsT=w1_codes[:, e, cols].bitcast(E4M3), lhsT_scale=w1_plane[:, e, cols],
+                rhs=da_codes[e][:].bitcast(E5M2), rhs_scale=da_plane[e][:], start=True, stop=True,
+            )
+            dx[e, b] = held.tile([P, C], F32, name=f"dx{e}{b}", tag=tag)
+            nc.scalar.copy(out=dx[e, b][:], in_=bank[:])
+
+        def scatter(e, b):
+            nc.vector.tensor_copy(window[b][:].indirect(expert_list(e)), dx[e, b][:])
+
+        for d in range(PACK):
+            nc.vector.scalar_tensor_tensor(
+                out=factor[:, d, :], in0=a0[d][:], scalar=0.0, in1=gates[0][:], op0=ALU.is_gt, op1=ALU.mult
+            )
+        for d in range(PACK):
+            gather(0, d, factor[:, d, :])
+        weave(0)
+        quantize(0, woven[0][:])
+        nc.sync.dma_start(out=a1, in_=a_rows[:, :, C : 2 * C])
+        for d in range(PACK):
+            gather(1, d, gates[1][:])
+        for b in range(3):
+            product(0, b)
+        weave(1)
+        sign = held.tile([P, C * PACK], BF16, name="sign", tag="late")
+        mask = held.tile([P, C * PACK], BF16, name="mask", tag="later")
+        masked = held.tile([P, C * PACK], BF16, name="masked", align_bytes=64)
+        nc.scalar.activation(woven_by_four(sign[:]), by_four(a1), ACT.Sign)
+        nc.scalar.activation(mask[:], sign[:], ACT.Relu)
+        nc.vector.tensor_tensor(masked[:], woven[1][:], mask[:], ALU.mult)
+        nc.tensor.matmul_mx(
+            out=banks[3][:], lhsT=w1_codes[:, 0, 3 * P : 4 * P].bitcast(E4M3), lhsT_scale=w1_plane[:, 0, 3 * P : 4 * P],
+            rhs=da_codes[0][:].bitcast(E5M2), rhs_scale=da_plane[0][:], start=True, stop=True,
+        )
+        quantize(1, masked[:])
+        half = C // 2
+        last = []
+        for h, tag in enumerate(("late", "later")):
+            part = held.tile([P, half], F32, name=f"dx03{h}", tag=tag)
+            nc.scalar.copy(out=part[:], in_=banks[3][:, h * half : (h + 1) * half])
+            last.append(part)
+        for b in range(4):
+            product(1, b)
+        for b in range(3):
+            scatter(0, b)
+        for h in range(2):
+            nc.vector.tensor_copy(window[3][:].indirect(offsets[:, h * half // 16 : (h + 1) * half // 16]), last[h][:])
+        for b in range(4):
+            scatter(1, b)
+        for b in range(4):
+            nc.sync.dma_start(out=out[b * P : (b + 1) * P, :], in_=window[b][:])

@@ -45,25 +45,23 @@ def tile_moe_sdb_relu_kernel(
         w2_zeroed = held.tile([P, H], U8, name="w2_zeroed", align_bytes=64)
         w2_codes = held.tile([P, H], I32, name="w2_codes", align_bytes=64)
         w2_plane = held.tile([P, H], U8, name="w2_plane", align_bytes=64)
-        dy_codes = held.tile([P, T], I32, name="dy_codes", align_bytes=64)
+        dy_codes = held.tile([P, T], I32, name="dy_codes", tag="dy", align_bytes=64)
         dy_plane = held.tile([P, T], U8, name="dy_plane", align_bytes=64)
         w1_codes = held.tile([P, E, K], I32, name="w1_codes", align_bytes=64)
         w1_plane = held.tile([P, E, K], U8, name="w1_plane", align_bytes=64)
         gates = [held.tile([P, C], F32, name=f"gate{e}") for e in range(E)]
         a0 = [held.tile([P, C], F32, name=f"a0{d}") for d in range(PACK)]
-        rows = held.tile([P, 10, C], F32, name="rows")
+        rows = held.tile([P, 8, C], F32, name="rows")
         factor = rows[:, 0:4, :]
         da = [rows[:, 4:8, :], rows[:, 2:6, :]]
-        a1 = rows[:, 6:10, :]
+        a1 = held.tile([P, PACK, C], F32, name="a1", tag="a1", align_bytes=64)
 
         nc.vector.memset(w2_zeroed[:].bitcast(I32), 0)
 
         load_scale_rows(nc.sync, w2_rows, w2t_scales[0])
         nc.sync.dma_start(out=w2_raw[:], in_=w2t_words[0].rearrange("p i d -> p (i d)").bitcast(I32))
         nc.sync.dma_start(out=dy_codes[:], in_=dy_words[0].rearrange("p t d -> p (t d)").bitcast(I32))
-        for r in range(4):
-            queue = nc.sync
-            queue.dma_start(out=dy_plane[r:P:32, :].bitcast(I32), in_=dy_scales[0][r:16:4, :].bitcast(I32))
+        load_scale_rows(nc.sync, dy_plane, dy_scales[0])
         a_rows = a.rearrange("(p d) s -> p d s", d=PACK)
         nc.sync.dma_start(out=gates[0][:], in_=gate[:, 0:C])
         nc.sync.dma_start(out=a0[0][:], in_=a_rows[:, 0, 0:C])
@@ -71,6 +69,7 @@ def tile_moe_sdb_relu_kernel(
         nc.sync.dma_start(offsets[:], offs)
         for d in range(2, PACK):
             nc.sync.dma_start(out=a0[d][:], in_=a_rows[:, d, 0:C])
+        nc.sync.dma_start(out=a1[:], in_=a_rows[:, :, C : 2 * C])
         nc.sync.dma_start(out=gates[1][:], in_=gate[:, C : 2 * C])
         nc.sync.dma_start(out=w1_codes[:], in_=w1t_words[:, 0].rearrange("e p k d -> p e (k d)").bitcast(I32))
         for r in range(4):
@@ -102,7 +101,12 @@ def tile_moe_sdb_relu_kernel(
                 )
                 nc.scalar.copy(out=dc[d][:, toks], in_=bank[:])
 
-        woven = [held.tile([P, C * PACK], BF16, name=f"woven{e}", align_bytes=64) for e in range(E)]
+        sign = held.tile([P, C * PACK], BF16, name="sign", tag="dy", align_bytes=64)
+        nc.scalar.activation(woven_by_four(sign[:]), by_four(a1[:]), ACT.Sign)
+        woven = [
+            held.tile([P, C * PACK], BF16, name="woven0", tag="a1", align_bytes=64),
+            held.tile([P, C * PACK], BF16, name="woven1", align_bytes=64),
+        ]
         da_codes = [held.tile([P, C], I32, name=f"da_codes{e}", align_bytes=64) for e in range(E)]
         da_plane = [held.tile([P, C], U8, name=f"da_plane{e}", align_bytes=64) for e in range(E)]
         window = [held.tile([P, T], F32, name=f"window{b}") for b in range(4)]
@@ -141,36 +145,21 @@ def tile_moe_sdb_relu_kernel(
             gather(0, d, factor[:, d, :])
         weave(0)
         quantize(0, woven[0][:])
-        nc.sync.dma_start(out=a1, in_=a_rows[:, :, C : 2 * C])
         for d in range(PACK):
             gather(1, d, gates[1][:])
         for b in range(3):
             product(0, b)
         weave(1)
-        sign = held.tile([P, C * PACK], BF16, name="sign", tag="late")
-        mask = held.tile([P, C * PACK], BF16, name="mask", tag="later")
+        mask = held.tile([P, C * PACK], BF16, name="mask", tag="late")
         masked = held.tile([P, C * PACK], BF16, name="masked", align_bytes=64)
-        nc.scalar.activation(woven_by_four(sign[:]), by_four(a1), ACT.Sign)
         nc.scalar.activation(mask[:], sign[:], ACT.Relu)
-        nc.vector.tensor_tensor(masked[:], woven[1][:], mask[:], ALU.mult)
-        nc.tensor.matmul_mx(
-            out=banks[3][:], lhsT=w1_codes[:, 0, 3 * P : 4 * P].bitcast(E4M3), lhsT_scale=w1_plane[:, 0, 3 * P : 4 * P],
-            rhs=da_codes[0][:].bitcast(E5M2), rhs_scale=da_plane[0][:], start=True, stop=True,
-        )
+        nc.gpsimd.tensor_tensor(masked[:], woven[1][:], mask[:], ALU.mult)
+        product(0, 3, tag="late")
         quantize(1, masked[:])
-        half = C // 2
-        last = []
-        for h, tag in enumerate(("late", "later")):
-            part = held.tile([P, half], F32, name=f"dx03{h}", tag=tag)
-            nc.scalar.copy(out=part[:], in_=banks[3][:, h * half : (h + 1) * half])
-            last.append(part)
         for b in range(4):
             product(1, b)
-        for b in range(3):
-            scatter(0, b)
-        for h in range(2):
-            nc.vector.tensor_copy(window[3][:].indirect(offsets[:, h * half // 16 : (h + 1) * half // 16]), last[h][:])
-        for b in range(4):
-            scatter(1, b)
+        for e in range(E):
+            for b in range(4):
+                scatter(e, b)
         for b in range(4):
             nc.sync.dma_start(out=out[b * P : (b + 1) * P, :], in_=window[b][:])

@@ -141,9 +141,18 @@ def tile_moe_sdb_relu_kernel(
             nc.vector.scalar_tensor_tensor(
                 out=factor[:, d, :], in0=a0[d][:], scalar=0.0, in1=gates[0][:], op0=ALU.is_gt, op1=ALU.mult
             )
-        for d in range(PACK):
+        for d in range(PACK - 1):
             gather(0, d, factor[:, d, :])
-        weave(0)
+        half = C // 2
+        for h in range(2):
+            slots = slice(h * half, (h + 1) * half)
+            nc.vector.tensor_tensor(
+                da[0][:, 3, slots], dc[3][:].indirect(offsets[:, h * half // 16 : (h + 1) * half // 16]),
+                factor[:, 3, slots], ALU.mult,
+            )
+            nc.scalar.copy(
+                out=woven_by_four(woven[0][:, h * half * PACK : (h + 1) * half * PACK]), in_=by_four(da[0][:, :, slots])
+            )
         quantize(0, woven[0][:])
         for d in range(PACK):
             gather(1, d, gates[1][:])

@@ -1,6 +1,7 @@
 from contextlib import ExitStack
 
 import concourse.mybir as mybir
+from concourse.masks import make_identity
 
 K, T, E, C, H, N = 512, 1024, 2, 512, 512, 512
 P = 128
@@ -49,28 +50,37 @@ def tile_moe_sdb_relu_kernel(
         dy_plane = held.tile([P, T], U8, name="dy_plane", align_bytes=64)
         w1_codes = held.tile([P, E, K], I32, name="w1_codes", align_bytes=64)
         w1_plane = held.tile([P, E, K], U8, name="w1_plane", align_bytes=64)
-        gates = [held.tile([P, C], F32, name=f"gate{e}") for e in range(E)]
+        gate_cols = held.tile([P, PACK], F32, name="gate_cols")
+        gate1 = held.tile([P, C], F32, name="gate1")
+        identity = held.tile([P, P], F32, name="identity")
+        banks = [psum.tile([P, C], F32, name=f"bank{b}") for b in range(8)]
         a0 = [held.tile([P, C], F32, name=f"a0{d}") for d in range(PACK)]
-        rows = held.tile([P, 8, C], F32, name="rows")
-        factor = rows[:, 0:4, :]
-        da = [rows[:, 4:8, :], rows[:, 2:6, :]]
+        rows = held.tile([P, 6 * C], F32, name="rows")
+        factor = [held.tile([P, C], F32, name=f"factor{d}")[:] for d in range(PACK - 1)]
+        factor.append(rows[:, 3 * C // 4 : C + 3 * C // 4])
+        da = [rows[:, first * C : (first + PACK) * C].rearrange("p (d s) -> p d s", d=PACK) for first in (2, 0)]
         a1 = held.tile([P, PACK, C], F32, name="a1", tag="a1", align_bytes=64)
 
         nc.vector.memset(w2_zeroed[:].bitcast(I32), 0)
+        nc.sync.dma_start(out=gate_cols[:], in_=gate[0, 0:C].rearrange("(p c) -> p c", c=PACK))
+        make_identity(nc, identity[:])
+        for c in range(PACK):
+            nc.tensor.transpose(
+                banks[7][:, c * P : (c + 1) * P], gate_cols[:, c : c + 1].to_broadcast([P, P]), identity[:]
+            )
+        gate0 = banks[7][:].rearrange("p (c n) -> p n c", c=PACK)
 
         load_scale_rows(nc.sync, w2_rows, w2t_scales[0])
         nc.sync.dma_start(out=w2_raw[:], in_=w2t_words[0].rearrange("p i d -> p (i d)").bitcast(I32))
+        a_rows = a.rearrange("(p d) s -> p d s", d=PACK)
+        nc.sync.dma_start(out=a0[0][:], in_=a_rows[:, 0, 0:C])
         nc.sync.dma_start(out=dy_codes[:], in_=dy_words[0].rearrange("p t d -> p (t d)").bitcast(I32))
         load_scale_rows(nc.sync, dy_plane, dy_scales[0])
-        a_rows = a.rearrange("(p d) s -> p d s", d=PACK)
-        nc.sync.dma_start(out=gates[0][:], in_=gate[:, 0:C])
-        nc.sync.dma_start(out=a0[0][:], in_=a_rows[:, 0, 0:C])
-        nc.sync.dma_start(out=a0[1][:], in_=a_rows[:, 1, 0:C])
-        nc.sync.dma_start(offsets[:], offs)
-        for d in range(2, PACK):
+        for d in range(1, PACK):
             nc.sync.dma_start(out=a0[d][:], in_=a_rows[:, d, 0:C])
+        nc.sync.dma_start(offsets[:], offs)
         nc.sync.dma_start(out=a1[:], in_=a_rows[:, :, C : 2 * C])
-        nc.sync.dma_start(out=gates[1][:], in_=gate[:, C : 2 * C])
+        nc.sync.dma_start(out=gate1[:], in_=gate[:, C : 2 * C])
         nc.sync.dma_start(out=w1_codes[:], in_=w1t_words[:, 0].rearrange("e p k d -> p e (k d)").bitcast(I32))
         for r in range(4):
             nc.sync.dma_start(
@@ -88,13 +98,12 @@ def tile_moe_sdb_relu_kernel(
             out=w2_plane[:].rearrange("p (d m) -> p d m", d=PACK), in_=w2_zeroed[:].rearrange("p (m d) -> p d m", d=PACK)
         )
 
-        banks = [psum.tile([P, C], F32, name=f"bank{b}") for b in range(8)]
         dc = [held.tile([P, T], F32, name=f"dc{d}") for d in range(PACK)]
         for d in range(PACK):
             cols = slice(d * P, (d + 1) * P)
             for h in range(2):
                 toks = slice(h * C, (h + 1) * C)
-                bank = banks[2 * d + h]
+                bank = banks[(2 * d + h) % 7]
                 nc.tensor.matmul_mx(
                     out=bank[:], lhsT=w2_codes[:, cols].bitcast(E4M3), lhsT_scale=w2_plane[:, cols],
                     rhs=dy_codes[:, toks].bitcast(E5M2), rhs_scale=dy_plane[:, toks], start=True, stop=True,
@@ -102,12 +111,20 @@ def tile_moe_sdb_relu_kernel(
                 nc.scalar.copy(out=dc[d][:, toks], in_=bank[:])
 
         sign = held.tile([P, C * PACK], BF16, name="sign", tag="dy", align_bytes=64)
-        nc.scalar.activation(woven_by_four(sign[:]), by_four(a1[:]), ACT.Sign)
+        half = C // 2
+
+        def sign_half(h):
+            nc.scalar.activation(
+                woven_by_four(sign[:, h * half * PACK : (h + 1) * half * PACK]),
+                by_four(a1[:, :, h * half : (h + 1) * half]), ACT.Sign,
+            )
+
+        sign_half(0)
         woven = [
-            held.tile([P, C * PACK], BF16, name="woven0", tag="a1", align_bytes=64),
+            held.tile([P, C * PACK], BF16, name="woven0", align_bytes=64),
             held.tile([P, C * PACK], BF16, name="woven1", align_bytes=64),
         ]
-        da_codes = [held.tile([P, C], I32, name=f"da_codes{e}", align_bytes=64) for e in range(E)]
+        da_codes = [held.tile([P, C], I32, name=f"da_codes{e}", tag=f"codes{e}", align_bytes=64) for e in range(E)]
         da_plane = [held.tile([P, C], U8, name=f"da_plane{e}", align_bytes=64) for e in range(E)]
         window = [held.tile([P, T], F32, name=f"window{b}") for b in range(4)]
         dx = {}
@@ -118,55 +135,64 @@ def tile_moe_sdb_relu_kernel(
         def gather(e, d, other):
             nc.vector.tensor_tensor(da[e][:, d, :], dc[d][:].indirect(expert_list(e)), other, ALU.mult)
 
-        def weave(e):
-            nc.scalar.copy(out=woven_by_four(woven[e][:]), in_=by_four(da[e]))
-
         def quantize(e, values):
             nc.vector.quantize_mx(out=da_codes[e][:].bitcast(E5M2), scales=da_plane[e][:], in_=values)
 
-        def product(e, b, tag=""):
+        def product(e, b):
             cols = slice(b * P, (b + 1) * P)
             bank = banks[4 * e + b]
             nc.tensor.matmul_mx(
                 out=bank[:], lhsT=w1_codes[:, e, cols].bitcast(E4M3), lhsT_scale=w1_plane[:, e, cols],
                 rhs=da_codes[e][:].bitcast(E5M2), rhs_scale=da_plane[e][:], start=True, stop=True,
             )
-            dx[e, b] = held.tile([P, C], F32, name=f"dx{e}{b}", tag=tag)
-            nc.scalar.copy(out=dx[e, b][:], in_=bank[:])
+
+        def evacuate(e, b, tag=""):
+            dx[e, b] = held.tile([P, C], F32, name=f"dx{e}{b}", tag=tag, align_bytes=64)
+            nc.scalar.copy(out=dx[e, b][:], in_=banks[4 * e + b][:])
 
         def scatter(e, b):
             nc.vector.tensor_copy(window[b][:].indirect(expert_list(e)), dx[e, b][:])
 
         for d in range(PACK):
             nc.vector.scalar_tensor_tensor(
-                out=factor[:, d, :], in0=a0[d][:], scalar=0.0, in1=gates[0][:], op0=ALU.is_gt, op1=ALU.mult
+                out=factor[d].rearrange("p (n c) -> p n c", c=PACK),
+                in0=a0[d][:].rearrange("p (n c) -> p n c", c=PACK),
+                scalar=0.0, in1=gate0, op0=ALU.is_gt, op1=ALU.mult,
             )
         for d in range(PACK - 1):
-            gather(0, d, factor[:, d, :])
-        half = C // 2
+            gather(0, d, factor[d])
         for h in range(2):
             slots = slice(h * half, (h + 1) * half)
             nc.vector.tensor_tensor(
                 da[0][:, 3, slots], dc[3][:].indirect(offsets[:, h * half // 16 : (h + 1) * half // 16]),
-                factor[:, 3, slots], ALU.mult,
+                factor[3][:, slots], ALU.mult,
             )
             nc.scalar.copy(
                 out=woven_by_four(woven[0][:, h * half * PACK : (h + 1) * half * PACK]), in_=by_four(da[0][:, :, slots])
             )
+        sign_half(1)
         quantize(0, woven[0][:])
         for d in range(PACK):
-            gather(1, d, gates[1][:])
-        for b in range(3):
+            gather(1, d, gate1[:])
+        values = [slice(h * half * PACK, (h + 1) * half * PACK) for h in range(2)]
+        mask_first = held.tile([P, half * PACK], BF16, name="mask_first")
+        nc.scalar.activation(mask_first[:], sign[:, values[0]], ACT.Relu)
+        for b in range(4):
             product(0, b)
-        weave(1)
-        mask = held.tile([P, C * PACK], BF16, name="mask", tag="late")
+        for b in range(3):
+            evacuate(0, b)
+        mask_second = held.tile([P, half * PACK], BF16, name="mask_second", tag="codes0", align_bytes=64)
         masked = held.tile([P, C * PACK], BF16, name="masked", align_bytes=64)
-        nc.scalar.activation(mask[:], sign[:], ACT.Relu)
-        nc.gpsimd.tensor_tensor(masked[:], woven[1][:], mask[:], ALU.mult)
-        product(0, 3, tag="late")
+        nc.scalar.copy(out=woven_by_four(woven[1][:, values[0]]), in_=by_four(da[1][:, :, 0:half]))
+        nc.gpsimd.tensor_tensor(masked[:, values[0]], woven[1][:, values[0]], mask_first[:], ALU.mult)
+        nc.scalar.activation(mask_second[:], sign[:, values[1]], ACT.Relu)
+        nc.scalar.copy(out=woven_by_four(woven[1][:, values[1]]), in_=by_four(da[1][:, :, half:C]))
+        nc.gpsimd.tensor_tensor(masked[:, values[1]], woven[1][:, values[1]], mask_second[:], ALU.mult)
+        evacuate(0, 3, tag="codes0")
         quantize(1, masked[:])
         for b in range(4):
             product(1, b)
+            evacuate(1, b)
         for e in range(E):
             for b in range(4):
                 scatter(e, b)

@@ -6,6 +6,9 @@ from concourse.masks import make_identity
 K, T, E, C, H, N = 512, 1024, 2, 512, 512, 512
 P = 128
 PACK = 4
+HALF = C // 2
+BLOCKS = K // P
+BANKS = 8
 FLOPS = 2 * N * H * T + 2 * H * K * E * C
 
 F32 = mybir.dt.float32
@@ -19,12 +22,12 @@ ALU = mybir.AluOpType
 ACT = mybir.ActivationFunctionType
 
 
-def load_scale_rows(queue, plane, rows):
+def load_scale_rows(nc, plane, rows):
     for r in range(4):
-        queue.dma_start(out=plane[r:P:32, :].bitcast(I32), in_=rows[r:16:4, :].bitcast(I32))
+        nc.sync.dma_start(out=plane[r:P:32, :].bitcast(I32), in_=rows[r:16:4, :].bitcast(I32))
 
 
-def by_four(ap):
+def strands_by_four(ap):
     return ap.rearrange("p d (c i) -> p c d i", i=4)
 
 
@@ -53,8 +56,9 @@ def tile_moe_sdb_relu_kernel(
         gate_cols = held.tile([P, PACK], F32, name="gate_cols")
         gate1 = held.tile([P, C], F32, name="gate1")
         identity = held.tile([P, P], F32, name="identity")
-        banks = [psum.tile([P, C], F32, name=f"bank{b}") for b in range(8)]
+        banks = [psum.tile([P, C], F32, name=f"bank{b}") for b in range(BANKS)]
         a0 = [held.tile([P, C], F32, name=f"a0{d}") for d in range(PACK)]
+
         rows = held.tile([P, 6 * C], F32, name="rows")
         factor = [held.tile([P, C], F32, name=f"factor{d}")[:] for d in range(PACK - 1)]
         factor.append(rows[:, 3 * C // 4 : C + 3 * C // 4])
@@ -62,20 +66,22 @@ def tile_moe_sdb_relu_kernel(
         a1 = held.tile([P, PACK, C], F32, name="a1", tag="a1", align_bytes=64)
 
         nc.vector.memset(w2_zeroed[:].bitcast(I32), 0)
+
         nc.sync.dma_start(out=gate_cols[:], in_=gate[0, 0:C].rearrange("(p c) -> p c", c=PACK))
         make_identity(nc, identity[:])
+        gate_bank = banks[BANKS - 1]
         for c in range(PACK):
             nc.tensor.transpose(
-                banks[7][:, c * P : (c + 1) * P], gate_cols[:, c : c + 1].to_broadcast([P, P]), identity[:]
+                gate_bank[:, c * P : (c + 1) * P], gate_cols[:, c : c + 1].to_broadcast([P, P]), identity[:]
             )
-        gate0 = banks[7][:].rearrange("p (c n) -> p n c", c=PACK)
+        gate0 = gate_bank[:].rearrange("p (c n) -> p n c", c=PACK)
 
-        load_scale_rows(nc.sync, w2_rows, w2t_scales[0])
         nc.sync.dma_start(out=w2_raw[:], in_=w2t_words[0].rearrange("p i d -> p (i d)").bitcast(I32))
+        load_scale_rows(nc, w2_rows, w2t_scales[0])
         a_rows = a.rearrange("(p d) s -> p d s", d=PACK)
         nc.sync.dma_start(out=a0[0][:], in_=a_rows[:, 0, 0:C])
         nc.sync.dma_start(out=dy_codes[:], in_=dy_words[0].rearrange("p t d -> p (t d)").bitcast(I32))
-        load_scale_rows(nc.sync, dy_plane, dy_scales[0])
+        load_scale_rows(nc, dy_plane, dy_scales[0])
         for d in range(1, PACK):
             nc.sync.dma_start(out=a0[d][:], in_=a_rows[:, d, 0:C])
         nc.sync.dma_start(offsets[:], offs)
@@ -103,30 +109,28 @@ def tile_moe_sdb_relu_kernel(
             cols = slice(d * P, (d + 1) * P)
             for h in range(2):
                 toks = slice(h * C, (h + 1) * C)
-                bank = banks[(2 * d + h) % 7]
+                bank = banks[(2 * d + h) % (BANKS - 1)]
                 nc.tensor.matmul_mx(
                     out=bank[:], lhsT=w2_codes[:, cols].bitcast(E4M3), lhsT_scale=w2_plane[:, cols],
                     rhs=dy_codes[:, toks].bitcast(E5M2), rhs_scale=dy_plane[:, toks], start=True, stop=True,
                 )
                 nc.scalar.copy(out=dc[d][:, toks], in_=bank[:])
 
+        half_slots = [slice(h * HALF, (h + 1) * HALF) for h in range(2)]
+        half_woven = [slice(h * HALF * PACK, (h + 1) * HALF * PACK) for h in range(2)]
+
         sign = held.tile([P, C * PACK], BF16, name="sign", tag="dy", align_bytes=64)
-        half = C // 2
 
         def sign_half(h):
             nc.scalar.activation(
-                woven_by_four(sign[:, h * half * PACK : (h + 1) * half * PACK]),
-                by_four(a1[:, :, h * half : (h + 1) * half]), ACT.Sign,
+                woven_by_four(sign[:, half_woven[h]]), strands_by_four(a1[:, :, half_slots[h]]), ACT.Sign
             )
 
         sign_half(0)
-        woven = [
-            held.tile([P, C * PACK], BF16, name="woven0", align_bytes=64),
-            held.tile([P, C * PACK], BF16, name="woven1", align_bytes=64),
-        ]
+        woven = [held.tile([P, C * PACK], BF16, name=f"woven{e}", align_bytes=64) for e in range(E)]
         da_codes = [held.tile([P, C], I32, name=f"da_codes{e}", tag=f"codes{e}", align_bytes=64) for e in range(E)]
         da_plane = [held.tile([P, C], U8, name=f"da_plane{e}", align_bytes=64) for e in range(E)]
-        window = [held.tile([P, T], F32, name=f"window{b}") for b in range(4)]
+        window = [held.tile([P, T], F32, name=f"window{b}") for b in range(BLOCKS)]
         dx = {}
 
         def expert_list(e):
@@ -135,20 +139,22 @@ def tile_moe_sdb_relu_kernel(
         def gather(e, d, other):
             nc.vector.tensor_tensor(da[e][:, d, :], dc[d][:].indirect(expert_list(e)), other, ALU.mult)
 
+        def weave_half(e, h):
+            nc.scalar.copy(out=woven_by_four(woven[e][:, half_woven[h]]), in_=strands_by_four(da[e][:, :, half_slots[h]]))
+
         def quantize(e, values):
             nc.vector.quantize_mx(out=da_codes[e][:].bitcast(E5M2), scales=da_plane[e][:], in_=values)
 
         def product(e, b):
             cols = slice(b * P, (b + 1) * P)
-            bank = banks[4 * e + b]
             nc.tensor.matmul_mx(
-                out=bank[:], lhsT=w1_codes[:, e, cols].bitcast(E4M3), lhsT_scale=w1_plane[:, e, cols],
+                out=banks[BLOCKS * e + b][:], lhsT=w1_codes[:, e, cols].bitcast(E4M3), lhsT_scale=w1_plane[:, e, cols],
                 rhs=da_codes[e][:].bitcast(E5M2), rhs_scale=da_plane[e][:], start=True, stop=True,
             )
 
         def evacuate(e, b, tag=""):
             dx[e, b] = held.tile([P, C], F32, name=f"dx{e}{b}", tag=tag, align_bytes=64)
-            nc.scalar.copy(out=dx[e, b][:], in_=banks[4 * e + b][:])
+            nc.scalar.copy(out=dx[e, b][:], in_=banks[BLOCKS * e + b][:])
 
         def scatter(e, b):
             nc.vector.tensor_copy(window[b][:].indirect(expert_list(e)), dx[e, b][:])
@@ -159,42 +165,43 @@ def tile_moe_sdb_relu_kernel(
                 in0=a0[d][:].rearrange("p (n c) -> p n c", c=PACK),
                 scalar=0.0, in1=gate0, op0=ALU.is_gt, op1=ALU.mult,
             )
-        for d in range(PACK - 1):
+        last_strand = PACK - 1
+        for d in range(last_strand):
             gather(0, d, factor[d])
         for h in range(2):
-            slots = slice(h * half, (h + 1) * half)
             nc.vector.tensor_tensor(
-                da[0][:, 3, slots], dc[3][:].indirect(offsets[:, h * half // 16 : (h + 1) * half // 16]),
-                factor[3][:, slots], ALU.mult,
+                da[0][:, last_strand, half_slots[h]],
+                dc[last_strand][:].indirect(offsets[:, h * HALF // 16 : (h + 1) * HALF // 16]),
+                factor[last_strand][:, half_slots[h]], ALU.mult,
             )
-            nc.scalar.copy(
-                out=woven_by_four(woven[0][:, h * half * PACK : (h + 1) * half * PACK]), in_=by_four(da[0][:, :, slots])
-            )
+            weave_half(0, h)
         sign_half(1)
         quantize(0, woven[0][:])
+
         for d in range(PACK):
             gather(1, d, gate1[:])
-        values = [slice(h * half * PACK, (h + 1) * half * PACK) for h in range(2)]
-        mask_first = held.tile([P, half * PACK], BF16, name="mask_first")
-        nc.scalar.activation(mask_first[:], sign[:, values[0]], ACT.Relu)
-        for b in range(4):
+        mask_first = held.tile([P, HALF * PACK], BF16, name="mask_first")
+        nc.scalar.activation(mask_first[:], sign[:, half_woven[0]], ACT.Relu)
+        last_block = BLOCKS - 1
+        for b in range(BLOCKS):
             product(0, b)
-        for b in range(3):
+        for b in range(last_block):
             evacuate(0, b)
-        mask_second = held.tile([P, half * PACK], BF16, name="mask_second", tag="codes0", align_bytes=64)
+        mask_second = held.tile([P, HALF * PACK], BF16, name="mask_second", tag="codes0", align_bytes=64)
         masked = held.tile([P, C * PACK], BF16, name="masked", align_bytes=64)
-        nc.scalar.copy(out=woven_by_four(woven[1][:, values[0]]), in_=by_four(da[1][:, :, 0:half]))
-        nc.gpsimd.tensor_tensor(masked[:, values[0]], woven[1][:, values[0]], mask_first[:], ALU.mult)
-        nc.scalar.activation(mask_second[:], sign[:, values[1]], ACT.Relu)
-        nc.scalar.copy(out=woven_by_four(woven[1][:, values[1]]), in_=by_four(da[1][:, :, half:C]))
-        nc.gpsimd.tensor_tensor(masked[:, values[1]], woven[1][:, values[1]], mask_second[:], ALU.mult)
-        evacuate(0, 3, tag="codes0")
+        weave_half(1, 0)
+        nc.gpsimd.tensor_tensor(masked[:, half_woven[0]], woven[1][:, half_woven[0]], mask_first[:], ALU.mult)
+        nc.scalar.activation(mask_second[:], sign[:, half_woven[1]], ACT.Relu)
+        weave_half(1, 1)
+        nc.gpsimd.tensor_tensor(masked[:, half_woven[1]], woven[1][:, half_woven[1]], mask_second[:], ALU.mult)
+        evacuate(0, last_block, tag="codes0")
         quantize(1, masked[:])
-        for b in range(4):
+        for b in range(BLOCKS):
             product(1, b)
             evacuate(1, b)
+
         for e in range(E):
-            for b in range(4):
+            for b in range(BLOCKS):
                 scatter(e, b)
-        for b in range(4):
+        for b in range(BLOCKS):
             nc.sync.dma_start(out=out[b * P : (b + 1) * P, :], in_=window[b][:])

@@ -22,9 +22,13 @@ ALU = mybir.AluOpType
 ACT = mybir.ActivationFunctionType
 
 
-def load_scale_rows(nc, plane, rows):
-    for r in range(4):
+def load_scale_rows(nc, plane, rows, which=range(4)):
+    for r in which:
         nc.sync.dma_start(out=plane[r:P:32, :].bitcast(I32), in_=rows[r:16:4, :].bitcast(I32))
+
+
+def load_quadrant_rows(nc, plane, rows, q):
+    nc.sync.dma_start(out=plane[32 * q : 32 * q + 4, :].bitcast(I32), in_=rows[4 * q : 4 * q + 4, :].bitcast(I32))
 
 
 def strands_by_four(ap):
@@ -76,13 +80,15 @@ def tile_moe_sdb_relu_kernel(
             )
         gate0 = gate_bank[:].rearrange("p (c n) -> p n c", c=PACK)
 
+        for q in range(3):
+            load_quadrant_rows(nc, w2_rows, w2t_scales[0], q)
         nc.sync.dma_start(out=w2_raw[:], in_=w2t_words[0].rearrange("p i d -> p (i d)").bitcast(I32))
-        load_scale_rows(nc, w2_rows, w2t_scales[0])
+        load_quadrant_rows(nc, w2_rows, w2t_scales[0], 3)
+        load_scale_rows(nc, dy_plane, dy_scales[0], range(1))
         a_rows = a.rearrange("(p d) s -> p d s", d=PACK)
-        nc.sync.dma_start(out=a0[0][:], in_=a_rows[:, 0, 0:C])
         nc.sync.dma_start(out=dy_codes[:], in_=dy_words[0].rearrange("p t d -> p (t d)").bitcast(I32))
-        load_scale_rows(nc, dy_plane, dy_scales[0])
-        for d in range(1, PACK):
+        load_scale_rows(nc, dy_plane, dy_scales[0], range(1, 4))
+        for d in range(PACK):
             nc.sync.dma_start(out=a0[d][:], in_=a_rows[:, d, 0:C])
         nc.sync.dma_start(offsets[:], offs)
         nc.sync.dma_start(out=a1[:], in_=a_rows[:, :, C : 2 * C])
@@ -98,10 +104,10 @@ def tile_moe_sdb_relu_kernel(
             live = slice(32 * q, 32 * q + 4)
             nc.vector.tensor_copy(out=w2_zeroed[live, :].bitcast(I32), in_=w2_rows[live, :].bitcast(I32))
         nc.vector.tensor_copy(
-            out=w2_codes[:].rearrange("p (d m) -> p d m", d=PACK), in_=w2_raw[:].rearrange("p (m d) -> p d m", d=PACK)
+            out=w2_plane[:].rearrange("p (d m) -> p d m", d=PACK), in_=w2_zeroed[:].rearrange("p (m d) -> p d m", d=PACK)
         )
         nc.vector.tensor_copy(
-            out=w2_plane[:].rearrange("p (d m) -> p d m", d=PACK), in_=w2_zeroed[:].rearrange("p (m d) -> p d m", d=PACK)
+            out=w2_codes[:].rearrange("p (d m) -> p d m", d=PACK), in_=w2_raw[:].rearrange("p (m d) -> p d m", d=PACK)
         )
 
         dc = [held.tile([P, T], F32, name=f"dc{d}") for d in range(PACK)]

@@ -58,15 +58,16 @@ def tile_moe_sdb_relu_kernel(
         w1_codes = held.tile([P, E, K], I32, name="w1_codes", align_bytes=64)
         w1_plane = held.tile([P, E, K], U8, name="w1_plane", align_bytes=64)
         gate_cols = held.tile([P, PACK], F32, name="gate_cols")
-        gate1 = held.tile([P, C], F32, name="gate1")
         identity = held.tile([P, P], F32, name="identity")
         banks = [psum.tile([P, C], F32, name=f"bank{b}") for b in range(BANKS)]
-        a0 = [held.tile([P, C], F32, name=f"a0{d}") for d in range(PACK)]
+        a0 = [held.tile([P, C - P], F32, name=f"a0{d}") for d in range(PACK)]
+        a_late = held.tile([P, PACK, P], F32, name="a_late")
 
-        rows = held.tile([P, 6 * C], F32, name="rows")
+        rows = held.tile([P, 8 * C], F32, name="rows")
         factor = [held.tile([P, C], F32, name=f"factor{d}")[:] for d in range(PACK - 1)]
         factor.append(rows[:, 3 * C // 4 : C + 3 * C // 4])
-        da = [rows[:, first * C : (first + PACK) * C].rearrange("p (d s) -> p d s", d=PACK) for first in (2, 0)]
+        da = [rows[:, first * C : (first + PACK) * C].rearrange("p (d s) -> p d s", d=PACK) for first in (4, 2)]
+        ungated = rows[:, 0 : 2 * C].rearrange("p (d s) -> p d s", d=2)
         a1 = held.tile([P, PACK, C], F32, name="a1", tag="a1", align_bytes=64)
 
         nc.vector.memset(w2_zeroed[:].bitcast(I32), 0)
@@ -79,6 +80,8 @@ def tile_moe_sdb_relu_kernel(
                 gate_bank[:, c * P : (c + 1) * P], gate_cols[:, c : c + 1].to_broadcast([P, P]), identity[:]
             )
         gate0 = gate_bank[:].rearrange("p (c n) -> p n c", c=PACK)
+        for d in range(PACK):
+            nc.scalar.copy(out=factor[d][:, 0:P].rearrange("p (n c) -> p n c", c=PACK), in_=gate0[:, 0 : P // PACK, :])
 
         for q in range(3):
             load_quadrant_rows(nc, w2_rows, w2t_scales[0], q)
@@ -89,10 +92,11 @@ def tile_moe_sdb_relu_kernel(
         nc.sync.dma_start(out=dy_codes[:], in_=dy_words[0].rearrange("p t d -> p (t d)").bitcast(I32))
         load_scale_rows(nc, dy_plane, dy_scales[0], range(1, 4))
         for d in range(PACK):
-            nc.sync.dma_start(out=a0[d][:], in_=a_rows[:, d, 0:C])
+            nc.sync.dma_start(out=a0[d][:], in_=a_rows[:, d, P:C])
         nc.sync.dma_start(offsets[:], offs)
+        nc.sync.dma_start(out=a_late[:], in_=a_rows[:, :, 0:P])
         nc.sync.dma_start(out=a1[:], in_=a_rows[:, :, C : 2 * C])
-        nc.sync.dma_start(out=gate1[:], in_=gate[:, C : 2 * C])
+        nc.sync.dma_start(out=da[1][:, 0:2, :], in_=gate[:, C : 2 * C].unsqueeze(1).to_broadcast([P, 2, C]))
         nc.sync.dma_start(out=w1_codes[:], in_=w1t_words[:, 0].rearrange("e p k d -> p e (k d)").bitcast(I32))
         for r in range(4):
             nc.sync.dma_start(
@@ -125,15 +129,15 @@ def tile_moe_sdb_relu_kernel(
         half_slots = [slice(h * HALF, (h + 1) * HALF) for h in range(2)]
         half_woven = [slice(h * HALF * PACK, (h + 1) * HALF * PACK) for h in range(2)]
 
-        sign = held.tile([P, C * PACK], BF16, name="sign", tag="dy", align_bytes=64)
+        sign_late = held.tile([P, P * PACK], BF16, name="sign_late", tag="dy", align_bytes=64)
+        nc.scalar.activation(woven_by_four(sign_late[:]), strands_by_four(a_late[:]), ACT.Sign)
+        mask_late = held.tile([P, P * PACK], BF16, name="mask_late", align_bytes=64)
+        nc.scalar.activation(mask_late[:], sign_late[:], ACT.Relu)
 
-        def sign_half(h):
-            nc.scalar.activation(
-                woven_by_four(sign[:, half_woven[h]]), strands_by_four(a1[:, :, half_slots[h]]), ACT.Sign
-            )
+        def sign_half(h, sign):
+            nc.scalar.activation(woven_by_four(sign), strands_by_four(a1[:, :, half_slots[h]]), ACT.Sign)
 
-        sign_half(0)
-        woven = [held.tile([P, C * PACK], BF16, name=f"woven{e}", align_bytes=64) for e in range(E)]
+        woven = [held.tile([P, C * PACK], BF16, name=f"woven{e}", tag=("dy", "")[e], align_bytes=64) for e in range(E)]
         da_codes = [held.tile([P, C], I32, name=f"da_codes{e}", tag=f"codes{e}", align_bytes=64) for e in range(E)]
         da_plane = [held.tile([P, C], U8, name=f"da_plane{e}", align_bytes=64) for e in range(E)]
         window = [held.tile([P, T], F32, name=f"window{b}") for b in range(BLOCKS)]
@@ -167,9 +171,9 @@ def tile_moe_sdb_relu_kernel(
 
         for d in range(PACK):
             nc.vector.scalar_tensor_tensor(
-                out=factor[d].rearrange("p (n c) -> p n c", c=PACK),
+                out=factor[d][:, P:C].rearrange("p (n c) -> p n c", c=PACK),
                 in0=a0[d][:].rearrange("p (n c) -> p n c", c=PACK),
-                scalar=0.0, in1=gate0, op0=ALU.is_gt, op1=ALU.mult,
+                scalar=0.0, in1=gate0[:, P // PACK :, :], op0=ALU.is_gt, op1=ALU.mult,
             )
         last_strand = PACK - 1
         for d in range(last_strand):
@@ -180,27 +184,43 @@ def tile_moe_sdb_relu_kernel(
                 dc[last_strand][:].indirect(offsets[:, h * HALF // 16 : (h + 1) * HALF // 16]),
                 factor[last_strand][:, half_slots[h]], ALU.mult,
             )
-            weave_half(0, h)
-        sign_half(1)
+            if h == 0:
+                for first in (0, P):
+                    nc.scalar.copy(
+                        out=woven_by_four(woven[0][:, first * PACK : (first + P) * PACK]),
+                        in_=strands_by_four(da[0][:, :, first : first + P]),
+                    )
+            else:
+                weave_half(0, h)
+        nc.gpsimd.tensor_tensor(woven[0][:, 0 : P * PACK], woven[0][:, 0 : P * PACK], mask_late[:], ALU.mult)
+        sign_first = rows[:, 7 * C : 8 * C].bitcast(BF16)
+        sign_half(0, sign_first)
         quantize(0, woven[0][:])
 
-        for d in range(PACK):
-            gather(1, d, gate1[:])
+        for d in range(2):
+            nc.vector.tensor_copy(ungated[:, d, :], dc[d][:].indirect(expert_list(1)))
+        for d in range(2, PACK):
+            gather(1, d, da[1][:, d - 2, :])
+        for h in range(2):
+            gated = da[1][:, 0:2, half_slots[h]]
+            nc.gpsimd.tensor_tensor(gated, ungated[:, :, half_slots[h]], gated, ALU.mult)
         mask_first = held.tile([P, HALF * PACK], BF16, name="mask_first")
-        nc.scalar.activation(mask_first[:], sign[:, half_woven[0]], ACT.Relu)
+        nc.scalar.activation(mask_first[:], sign_first, ACT.Relu)
         last_block = BLOCKS - 1
         for b in range(BLOCKS):
             product(0, b)
         for b in range(last_block):
             evacuate(0, b)
-        mask_second = held.tile([P, HALF * PACK], BF16, name="mask_second", tag="codes0", align_bytes=64)
+        mask_second = held.tile([P, HALF * PACK], BF16, name="mask_second", tag="mask_second", align_bytes=64)
         masked = held.tile([P, C * PACK], BF16, name="masked", align_bytes=64)
+        sign_second = held.tile([P, HALF * PACK], BF16, name="sign_second", tag="codes0", align_bytes=64)
+        sign_half(1, sign_second[:])
         weave_half(1, 0)
         nc.gpsimd.tensor_tensor(masked[:, half_woven[0]], woven[1][:, half_woven[0]], mask_first[:], ALU.mult)
-        nc.scalar.activation(mask_second[:], sign[:, half_woven[1]], ACT.Relu)
+        nc.scalar.activation(mask_second[:], sign_second[:], ACT.Relu)
         weave_half(1, 1)
         nc.gpsimd.tensor_tensor(masked[:, half_woven[1]], woven[1][:, half_woven[1]], mask_second[:], ALU.mult)
-        evacuate(0, last_block, tag="codes0")
+        evacuate(0, last_block, tag="mask_second")
         quantize(1, masked[:])
         for b in range(BLOCKS):
             product(1, b)

@@ -7,6 +7,7 @@ K, T, E, C, H, N = 512, 1024, 2, 512, 512, 512
 P = 128
 PACK = 4
 HALF = C // 2
+LATE = 96
 BLOCKS = K // P
 BANKS = 8
 FLOPS = 2 * N * H * T + 2 * H * K * E * C
@@ -60,8 +61,8 @@ def tile_moe_sdb_relu_kernel(
         gate_cols = held.tile([P, PACK], F32, name="gate_cols")
         identity = held.tile([P, P], F32, name="identity")
         banks = [psum.tile([P, C], F32, name=f"bank{b}") for b in range(BANKS)]
-        a0 = [held.tile([P, C - P], F32, name=f"a0{d}") for d in range(PACK)]
-        a_late = held.tile([P, PACK, P], F32, name="a_late")
+        a0 = [held.tile([P, C - LATE], F32, name=f"a0{d}") for d in range(PACK)]
+        a_late = held.tile([P, PACK, LATE], F32, name="a_late")
 
         rows = held.tile([P, 8 * C], F32, name="rows")
         factor = [held.tile([P, C], F32, name=f"factor{d}")[:] for d in range(PACK - 1)]
@@ -81,7 +82,7 @@ def tile_moe_sdb_relu_kernel(
             )
         gate0 = gate_bank[:].rearrange("p (c n) -> p n c", c=PACK)
         for d in range(PACK):
-            nc.scalar.copy(out=factor[d][:, 0:P].rearrange("p (n c) -> p n c", c=PACK), in_=gate0[:, 0 : P // PACK, :])
+            nc.scalar.copy(out=factor[d][:, 0:LATE].rearrange("p (n c) -> p n c", c=PACK), in_=gate0[:, 0 : LATE // PACK, :])
 
         for q in range(3):
             load_quadrant_rows(nc, w2_rows, w2t_scales[0], q)
@@ -92,9 +93,9 @@ def tile_moe_sdb_relu_kernel(
         nc.sync.dma_start(out=dy_codes[:], in_=dy_words[0].rearrange("p t d -> p (t d)").bitcast(I32))
         load_scale_rows(nc, dy_plane, dy_scales[0], range(1, 4))
         for d in range(PACK):
-            nc.sync.dma_start(out=a0[d][:], in_=a_rows[:, d, P:C])
+            nc.sync.dma_start(out=a0[d][:], in_=a_rows[:, d, LATE:C])
         nc.sync.dma_start(offsets[:], offs)
-        nc.sync.dma_start(out=a_late[:], in_=a_rows[:, :, 0:P])
+        nc.sync.dma_start(out=a_late[:], in_=a_rows[:, :, 0:LATE])
         nc.sync.dma_start(out=a1[:], in_=a_rows[:, :, C : 2 * C])
         nc.sync.dma_start(out=da[1][:, 0:2, :], in_=gate[:, C : 2 * C].unsqueeze(1).to_broadcast([P, 2, C]))
         nc.sync.dma_start(out=w1_codes[:], in_=w1t_words[:, 0].rearrange("e p k d -> p e (k d)").bitcast(I32))
@@ -129,9 +130,9 @@ def tile_moe_sdb_relu_kernel(
         half_slots = [slice(h * HALF, (h + 1) * HALF) for h in range(2)]
         half_woven = [slice(h * HALF * PACK, (h + 1) * HALF * PACK) for h in range(2)]
 
-        sign_late = held.tile([P, P * PACK], BF16, name="sign_late", tag="dy", align_bytes=64)
+        sign_late = held.tile([P, LATE * PACK], BF16, name="sign_late", tag="dy", align_bytes=64)
         nc.scalar.activation(woven_by_four(sign_late[:]), strands_by_four(a_late[:]), ACT.Sign)
-        mask_late = held.tile([P, P * PACK], BF16, name="mask_late", align_bytes=64)
+        mask_late = held.tile([P, LATE * PACK], BF16, name="mask_late", align_bytes=64)
         nc.scalar.activation(mask_late[:], sign_late[:], ACT.Relu)
 
         def sign_half(h, sign):
@@ -139,7 +140,7 @@ def tile_moe_sdb_relu_kernel(
 
         woven = [held.tile([P, C * PACK], BF16, name=f"woven{e}", tag=("dy", "")[e], align_bytes=64) for e in range(E)]
         da_codes = [held.tile([P, C], I32, name=f"da_codes{e}", tag=f"codes{e}", align_bytes=64) for e in range(E)]
-        da_plane = [held.tile([P, C], U8, name=f"da_plane{e}", align_bytes=64) for e in range(E)]
+        da_plane = [held.tile([P, C], U8, name=f"da_plane{e}", tag=f"plane{e}", align_bytes=64) for e in range(E)]
         window = [held.tile([P, T], F32, name=f"window{b}") for b in range(BLOCKS)]
         dx = {}
 
@@ -171,9 +172,9 @@ def tile_moe_sdb_relu_kernel(
 
         for d in range(PACK):
             nc.vector.scalar_tensor_tensor(
-                out=factor[d][:, P:C].rearrange("p (n c) -> p n c", c=PACK),
+                out=factor[d][:, LATE:C].rearrange("p (n c) -> p n c", c=PACK),
                 in0=a0[d][:].rearrange("p (n c) -> p n c", c=PACK),
-                scalar=0.0, in1=gate0[:, P // PACK :, :], op0=ALU.is_gt, op1=ALU.mult,
+                scalar=0.0, in1=gate0[:, LATE // PACK :, :], op0=ALU.is_gt, op1=ALU.mult,
             )
         last_strand = PACK - 1
         for d in range(last_strand):
@@ -185,14 +186,14 @@ def tile_moe_sdb_relu_kernel(
                 factor[last_strand][:, half_slots[h]], ALU.mult,
             )
             if h == 0:
-                for first in (0, P):
+                for first, stop in ((0, LATE), (LATE, HALF)):
                     nc.scalar.copy(
-                        out=woven_by_four(woven[0][:, first * PACK : (first + P) * PACK]),
-                        in_=strands_by_four(da[0][:, :, first : first + P]),
+                        out=woven_by_four(woven[0][:, first * PACK : stop * PACK]),
+                        in_=strands_by_four(da[0][:, :, first:stop]),
                     )
             else:
                 weave_half(0, h)
-        nc.gpsimd.tensor_tensor(woven[0][:, 0 : P * PACK], woven[0][:, 0 : P * PACK], mask_late[:], ALU.mult)
+        nc.gpsimd.tensor_tensor(woven[0][:, 0 : LATE * PACK], woven[0][:, 0 : LATE * PACK], mask_late[:], ALU.mult)
         sign_first = rows[:, 7 * C : 8 * C].bitcast(BF16)
         sign_half(0, sign_first)
         quantize(0, woven[0][:])
@@ -204,16 +205,17 @@ def tile_moe_sdb_relu_kernel(
         for h in range(2):
             gated = da[1][:, 0:2, half_slots[h]]
             nc.gpsimd.tensor_tensor(gated, ungated[:, :, half_slots[h]], gated, ALU.mult)
-        mask_first = held.tile([P, HALF * PACK], BF16, name="mask_first")
-        nc.scalar.activation(mask_first[:], sign_first, ACT.Relu)
         last_block = BLOCKS - 1
         for b in range(BLOCKS):
             product(0, b)
-        for b in range(last_block):
+        evacuate(0, 0)
+        mask_first = held.tile([P, HALF * PACK], BF16, name="mask_first", tag="codes0", align_bytes=64)
+        nc.scalar.activation(mask_first[:], sign_first, ACT.Relu)
+        for b in range(1, last_block):
             evacuate(0, b)
         mask_second = held.tile([P, HALF * PACK], BF16, name="mask_second", tag="mask_second", align_bytes=64)
         masked = held.tile([P, C * PACK], BF16, name="masked", align_bytes=64)
-        sign_second = held.tile([P, HALF * PACK], BF16, name="sign_second", tag="codes0", align_bytes=64)
+        sign_second = held.tile([P, HALF * PACK], BF16, name="sign_second", tag="plane0", align_bytes=64)
         sign_half(1, sign_second[:])
         weave_half(1, 0)
         nc.gpsimd.tensor_tensor(masked[:, half_woven[0]], woven[1][:, half_woven[0]], mask_first[:], ALU.mult)

@@ -135,8 +135,8 @@ def tile_moe_sdb_relu_kernel(
         mask_late = held.tile([P, LATE * PACK], BF16, name="mask_late", align_bytes=64)
         nc.scalar.activation(mask_late[:], sign_late[:], ACT.Relu)
 
-        def sign_half(h, sign):
-            nc.scalar.activation(woven_by_four(sign), strands_by_four(a1[:, :, half_slots[h]]), ACT.Sign)
+        def sign_of(first, count, sign):
+            nc.scalar.activation(woven_by_four(sign), strands_by_four(a1[:, :, first : first + count]), ACT.Sign)
 
         woven = [held.tile([P, C * PACK], BF16, name=f"woven{e}", tag=("dy", "")[e], align_bytes=64) for e in range(E)]
         da_codes = [held.tile([P, C], I32, name=f"da_codes{e}", tag=f"codes{e}", align_bytes=64) for e in range(E)]
@@ -195,7 +195,9 @@ def tile_moe_sdb_relu_kernel(
                 weave_half(0, h)
         nc.gpsimd.tensor_tensor(woven[0][:, 0 : LATE * PACK], woven[0][:, 0 : LATE * PACK], mask_late[:], ALU.mult)
         sign_first = rows[:, 7 * C : 8 * C].bitcast(BF16)
-        sign_half(0, sign_first)
+        sign_of(0, HALF, sign_first)
+        sign_third = rows[:, 6 * C : 6 * C + HALF].bitcast(BF16)
+        sign_of(HALF, P, sign_third)
         quantize(0, woven[0][:])
 
         for d in range(2):
@@ -209,20 +211,20 @@ def tile_moe_sdb_relu_kernel(
         for b in range(BLOCKS):
             product(0, b)
         evacuate(0, 0)
-        mask_first = held.tile([P, HALF * PACK], BF16, name="mask_first", tag="codes0", align_bytes=64)
-        nc.scalar.activation(mask_first[:], sign_first, ACT.Relu)
-        for b in range(1, last_block):
-            evacuate(0, b)
-        mask_second = held.tile([P, HALF * PACK], BF16, name="mask_second", tag="mask_second", align_bytes=64)
+        mask = held.tile([P, C * PACK], BF16, name="mask", tag="codes0", align_bytes=64)
+        nc.scalar.activation(mask[:, half_woven[0]], sign_first, ACT.Relu)
+        evacuate(0, 1)
         masked = held.tile([P, C * PACK], BF16, name="masked", align_bytes=64)
-        sign_second = held.tile([P, HALF * PACK], BF16, name="sign_second", tag="plane0", align_bytes=64)
-        sign_half(1, sign_second[:])
+        sign_fourth = held.tile([P, P * PACK], BF16, name="sign_fourth", tag="plane0", align_bytes=64)
+        sign_of(HALF + P, P, sign_fourth[:])
         weave_half(1, 0)
-        nc.gpsimd.tensor_tensor(masked[:, half_woven[0]], woven[1][:, half_woven[0]], mask_first[:], ALU.mult)
-        nc.scalar.activation(mask_second[:], sign_second[:], ACT.Relu)
+        nc.gpsimd.tensor_tensor(masked[:, half_woven[0]], woven[1][:, half_woven[0]], mask[:, half_woven[0]], ALU.mult)
+        nc.scalar.activation(mask[:, HALF * PACK : (HALF + P) * PACK], sign_third, ACT.Relu)
+        nc.scalar.activation(mask[:, (HALF + P) * PACK : C * PACK], sign_fourth[:], ACT.Relu)
         weave_half(1, 1)
-        nc.gpsimd.tensor_tensor(masked[:, half_woven[1]], woven[1][:, half_woven[1]], mask_second[:], ALU.mult)
-        evacuate(0, last_block, tag="mask_second")
+        evacuate(0, 2)
+        nc.gpsimd.tensor_tensor(masked[:, half_woven[1]], woven[1][:, half_woven[1]], mask[:, half_woven[1]], ALU.mult)
+        evacuate(0, last_block, tag="codes0")
         quantize(1, masked[:])
         for b in range(BLOCKS):
             product(1, b)

@@ -6,8 +6,8 @@ from concourse.masks import make_identity
 K, T, E, C, H, N = 512, 1024, 2, 512, 512, 512
 P = 128
 PACK = 4
-HALF = C // 2
-LATE = 96
+GROUP = 256
+GROUPS = E * C // GROUP
 BLOCKS = K // P
 BANKS = 8
 FLOPS = 2 * N * H * T + 2 * H * K * E * C
@@ -15,21 +15,13 @@ FLOPS = 2 * N * H * T + 2 * H * K * E * C
 F32 = mybir.dt.float32
 BF16 = mybir.dt.bfloat16
 I32 = mybir.dt.int32
+U32 = mybir.dt.uint32
 U16 = mybir.dt.uint16
 U8 = mybir.dt.uint8
 E4M3 = mybir.dt.float8_e4m3fn_x4
 E5M2 = mybir.dt.float8_e5m2_x4
 ALU = mybir.AluOpType
 ACT = mybir.ActivationFunctionType
-
-
-def load_scale_rows(nc, plane, rows, which=range(4)):
-    for r in which:
-        nc.sync.dma_start(out=plane[r:P:32, :].bitcast(I32), in_=rows[r:16:4, :].bitcast(I32))
-
-
-def load_quadrant_rows(nc, plane, rows, q):
-    nc.sync.dma_start(out=plane[32 * q : 32 * q + 4, :].bitcast(I32), in_=rows[4 * q : 4 * q + 4, :].bitcast(I32))
 
 
 def strands_by_four(ap):
@@ -46,34 +38,49 @@ def tile_moe_sdb_relu_kernel(
     nc = tc.nc
     with ExitStack() as ctx:
         held = ctx.enter_context(tc.tile_pool(name="held", bufs=1))
+        placed = ctx.enter_context(tc.tile_pool(name="placed", bufs=1))
         psum = ctx.enter_context(tc.psum_pool(name="psum", bufs=1))
 
         offsets = held.tile([P, E * C // 16], U16, name="offsets")
         w2_raw = held.tile([P, H], I32, name="w2_raw", align_bytes=64)
-        w2_rows = held.tile([P, H], U8, name="w2_rows", align_bytes=64)
+        w2_rows = held.tile([4, 4, H], U8, name="w2_rows", align_bytes=64)
         w2_zeroed = held.tile([P, H], U8, name="w2_zeroed", align_bytes=64)
         w2_codes = held.tile([P, H], I32, name="w2_codes", align_bytes=64)
-        w2_plane = held.tile([P, H], U8, name="w2_plane", align_bytes=64)
-        dy_codes = held.tile([P, T], I32, name="dy_codes", tag="dy", align_bytes=64)
-        dy_plane = held.tile([P, T], U8, name="dy_plane", align_bytes=64)
+        dy_codes = [held.tile([P, C], I32, name=f"dy_codes{h}", tag=f"dy{h}", align_bytes=64) for h in range(2)]
+        dy_rows = held.tile([P, 4, T], U8, name="dy_rows", align_bytes=64)
+        dy_plane = dy_rows[:, 0, :]
         w1_codes = held.tile([P, E, K], I32, name="w1_codes", align_bytes=64)
         w1_plane = held.tile([P, E, K], U8, name="w1_plane", align_bytes=64)
-        gate_cols = held.tile([P, PACK], F32, name="gate_cols")
+        gate_cols = held.tile([P, PACK], F32, name="gate_cols", tag="gate_cols", align_bytes=64)
+        gate1 = held.tile([P, C], F32, name="gate1")
         identity = held.tile([P, P], F32, name="identity")
         banks = [psum.tile([P, C], F32, name=f"bank{b}") for b in range(BANKS)]
-        a0 = [held.tile([P, C - LATE], F32, name=f"a0{d}") for d in range(PACK)]
-        a_late = held.tile([P, PACK, LATE], F32, name="a_late")
-
-        rows = held.tile([P, 8 * C], F32, name="rows")
-        factor = [held.tile([P, C], F32, name=f"factor{d}")[:] for d in range(PACK - 1)]
-        factor.append(rows[:, 3 * C // 4 : C + 3 * C // 4])
-        da = [rows[:, first * C : (first + PACK) * C].rearrange("p (d s) -> p d s", d=PACK) for first in (4, 2)]
-        ungated = rows[:, 0 : 2 * C].rearrange("p (d s) -> p d s", d=2)
-        a1 = held.tile([P, PACK, C], F32, name="a1", tag="a1", align_bytes=64)
+        a0 = [held.tile([P, C], F32, name=f"a0{d}") for d in range(PACK)]
+        a1 = held.tile([P, PACK, C], F32, name="a1")
 
         nc.vector.memset(w2_zeroed[:].bitcast(I32), 0)
 
+        a_rows = a.rearrange("(p d) s -> p d s", d=PACK)
         nc.sync.dma_start(out=gate_cols[:], in_=gate[0, 0:C].rearrange("(p c) -> p c", c=PACK))
+        nc.sync.dma_start(out=w2_rows[:].bitcast(I32), in_=w2t_scales[0].rearrange("(q r) i -> r q i", r=4).bitcast(I32))
+        nc.sync.dma_start(out=dy_rows[0:4].bitcast(I32), in_=dy_scales[0].rearrange("(q r) t -> r q t", r=4).bitcast(I32))
+        nc.sync.dma_start(out=w2_raw[:], in_=w2t_words[0].rearrange("p i d -> p (i d)").bitcast(I32))
+        dy_flat = dy_words[0].rearrange("p t d -> p (t d)").bitcast(I32)
+        for h in range(2):
+            nc.sync.dma_start(out=dy_codes[h][:], in_=dy_flat[:, h * C : (h + 1) * C])
+        nc.sync.dma_start(out=a0[0][:], in_=a_rows[:, 0, 0:C])
+        nc.sync.dma_start(offsets[:], offs)
+        for d in range(1, PACK):
+            nc.sync.dma_start(out=a0[d][:], in_=a_rows[:, d, 0:C])
+        nc.sync.dma_start(out=w1_codes[:], in_=w1t_words[:, 0].rearrange("e p k d -> p e (k d)").bitcast(I32))
+        for r in range(4):
+            nc.sync.dma_start(
+                out=w1_plane[r:P:32, :, :].bitcast(I32),
+                in_=w1t_scales[:, 0, r:16:4, :].rearrange("e q k -> q e k").bitcast(I32),
+            )
+        nc.sync.dma_start(out=a1[:], in_=a_rows[:, :, C : 2 * C])
+        nc.sync.dma_start(out=gate1[:], in_=gate[:, C : 2 * C])
+
         make_identity(nc, identity[:])
         gate_bank = banks[BANKS - 1]
         for c in range(PACK):
@@ -81,38 +88,19 @@ def tile_moe_sdb_relu_kernel(
                 gate_bank[:, c * P : (c + 1) * P], gate_cols[:, c : c + 1].to_broadcast([P, P]), identity[:]
             )
         gate0 = gate_bank[:].rearrange("p (c n) -> p n c", c=PACK)
-        for d in range(PACK):
-            nc.scalar.copy(out=factor[d][:, 0:LATE].rearrange("p (n c) -> p n c", c=PACK), in_=gate0[:, 0 : LATE // PACK, :])
-
-        for q in range(3):
-            load_quadrant_rows(nc, w2_rows, w2t_scales[0], q)
-        nc.sync.dma_start(out=w2_raw[:], in_=w2t_words[0].rearrange("p i d -> p (i d)").bitcast(I32))
-        load_quadrant_rows(nc, w2_rows, w2t_scales[0], 3)
-        load_scale_rows(nc, dy_plane, dy_scales[0], range(1))
-        a_rows = a.rearrange("(p d) s -> p d s", d=PACK)
-        nc.sync.dma_start(out=dy_codes[:], in_=dy_words[0].rearrange("p t d -> p (t d)").bitcast(I32))
-        load_scale_rows(nc, dy_plane, dy_scales[0], range(1, 4))
-        for d in range(PACK):
-            nc.sync.dma_start(out=a0[d][:], in_=a_rows[:, d, LATE:C])
-        nc.sync.dma_start(offsets[:], offs)
-        nc.sync.dma_start(out=a_late[:], in_=a_rows[:, :, 0:LATE])
-        nc.sync.dma_start(out=a1[:], in_=a_rows[:, :, C : 2 * C])
-        nc.sync.dma_start(out=da[1][:, 0:2, :], in_=gate[:, C : 2 * C].unsqueeze(1).to_broadcast([P, 2, C]))
-        nc.sync.dma_start(out=w1_codes[:], in_=w1t_words[:, 0].rearrange("e p k d -> p e (k d)").bitcast(I32))
-        for r in range(4):
-            nc.sync.dma_start(
-                out=w1_plane[r:P:32, :, :].bitcast(I32),
-                in_=w1t_scales[:, 0, r:16:4, :].rearrange("e q k -> q e k").bitcast(I32),
-            )
 
         for q in range(4):
-            live = slice(32 * q, 32 * q + 4)
-            nc.vector.tensor_copy(out=w2_zeroed[live, :].bitcast(I32), in_=w2_rows[live, :].bitcast(I32))
+            nc.vector.tensor_copy(out=w2_zeroed[32 * q : 32 * q + 4, :].bitcast(I32), in_=w2_rows[:, q, :].bitcast(I32))
+        w2_plane = held.tile([P, H], U8, name="w2_plane", tag="gate_cols", align_bytes=64)
         nc.vector.tensor_copy(
-            out=w2_plane[:].rearrange("p (d m) -> p d m", d=PACK), in_=w2_zeroed[:].rearrange("p (m d) -> p d m", d=PACK)
+            out=w2_plane[:].rearrange("p (d c i) -> p c d i", d=PACK, i=16),
+            in_=w2_zeroed[:].rearrange("p (c i d) -> p c d i", d=PACK, i=16),
         )
-        nc.vector.tensor_copy(
-            out=w2_codes[:].rearrange("p (d m) -> p d m", d=PACK), in_=w2_raw[:].rearrange("p (m d) -> p d m", d=PACK)
+        for q in range(1, 4):
+            nc.vector.tensor_copy(out=dy_plane[32 * q : 32 * q + 4, :].bitcast(I32), in_=dy_rows[0:4, q, :].bitcast(I32))
+        nc.scalar.copy(
+            out=w2_codes[:].bitcast(U32).rearrange("p (d c i) -> p c d i", d=PACK, i=4),
+            in_=w2_raw[:].bitcast(U32).rearrange("p (c i d) -> p c d i", d=PACK, i=4),
         )
 
         dc = [held.tile([P, T], F32, name=f"dc{d}") for d in range(PACK)]
@@ -123,115 +111,120 @@ def tile_moe_sdb_relu_kernel(
                 bank = banks[(2 * d + h) % (BANKS - 1)]
                 nc.tensor.matmul_mx(
                     out=bank[:], lhsT=w2_codes[:, cols].bitcast(E4M3), lhsT_scale=w2_plane[:, cols],
-                    rhs=dy_codes[:, toks].bitcast(E5M2), rhs_scale=dy_plane[:, toks], start=True, stop=True,
+                    rhs=dy_codes[h][:].bitcast(E5M2), rhs_scale=dy_plane[:, toks], start=True, stop=True,
                 )
                 nc.scalar.copy(out=dc[d][:, toks], in_=bank[:])
 
-        half_slots = [slice(h * HALF, (h + 1) * HALF) for h in range(2)]
-        half_woven = [slice(h * HALF * PACK, (h + 1) * HALF * PACK) for h in range(2)]
+        def slots(first, count):
+            return offsets[:, first // 16 : (first + count) // 16]
 
-        sign_late = held.tile([P, LATE * PACK], BF16, name="sign_late", tag="dy", align_bytes=64)
-        nc.scalar.activation(woven_by_four(sign_late[:]), strands_by_four(a_late[:]), ACT.Sign)
-        mask_late = held.tile([P, LATE * PACK], BF16, name="mask_late", align_bytes=64)
-        nc.scalar.activation(mask_late[:], sign_late[:], ACT.Relu)
-
-        def sign_of(first, count, sign):
-            nc.scalar.activation(woven_by_four(sign), strands_by_four(a1[:, :, first : first + count]), ACT.Sign)
-
-        woven = [held.tile([P, C * PACK], BF16, name=f"woven{e}", tag=("dy", "")[e], align_bytes=64) for e in range(E)]
-        da_codes = [held.tile([P, C], I32, name=f"da_codes{e}", tag=f"codes{e}", align_bytes=64) for e in range(E)]
-        da_plane = [held.tile([P, C], U8, name=f"da_plane{e}", tag=f"plane{e}", align_bytes=64) for e in range(E)]
         window = [held.tile([P, T], F32, name=f"window{b}") for b in range(BLOCKS)]
-        dx = {}
+        codes = [held.tile([P, C], I32, name=f"codes{e}", align_bytes=64) for e in range(E)]
+        plane = [held.tile([P, C], U8, name=f"plane{e}", align_bytes=64) for e in range(E)]
+        da0 = held.tile([P, PACK, C], F32, name="da0")
+        picked = held.tile([P, PACK, C], F32, name="picked", tag="dy1", align_bytes=64)
+        halves = [slice(0, GROUP), slice(GROUP, C)]
 
-        def expert_list(e):
-            return offsets[:, e * C // 16 : (e + 1) * C // 16]
-
-        def gather(e, d, other):
-            nc.vector.tensor_tensor(da[e][:, d, :], dc[d][:].indirect(expert_list(e)), other, ALU.mult)
-
-        def weave_half(e, h):
-            nc.scalar.copy(out=woven_by_four(woven[e][:, half_woven[h]]), in_=strands_by_four(da[e][:, :, half_slots[h]]))
-
-        def quantize(e, values):
-            nc.vector.quantize_mx(out=da_codes[e][:].bitcast(E5M2), scales=da_plane[e][:], in_=values)
-
-        def product(e, b):
-            cols = slice(b * P, (b + 1) * P)
+        def product(e, b, cols, dst):
+            rows = slice(b * P, (b + 1) * P)
             nc.tensor.matmul_mx(
-                out=banks[BLOCKS * e + b][:], lhsT=w1_codes[:, e, cols].bitcast(E4M3), lhsT_scale=w1_plane[:, e, cols],
-                rhs=da_codes[e][:].bitcast(E5M2), rhs_scale=da_plane[e][:], start=True, stop=True,
+                out=dst, lhsT=w1_codes[:, e, rows].bitcast(E4M3), lhsT_scale=w1_plane[:, e, rows],
+                rhs=codes[e][:, cols].bitcast(E5M2), rhs_scale=plane[e][:, cols], start=True, stop=True,
             )
 
-        def evacuate(e, b, tag=""):
-            dx[e, b] = held.tile([P, C], F32, name=f"dx{e}{b}", tag=tag, align_bytes=64)
-            nc.scalar.copy(out=dx[e, b][:], in_=banks[BLOCKS * e + b][:])
+        def vector_bank(e, b):
+            return banks[4 * e + b]
 
-        def scatter(e, b):
-            nc.vector.tensor_copy(window[b][:].indirect(expert_list(e)), dx[e, b][:])
+        def scalar_bank(e, h):
+            return banks[4 * e + 2 + h]
 
+        def quantize(e, h, woven):
+            nc.vector.quantize_mx(out=codes[e][:, halves[h]].bitcast(E5M2), scales=plane[e][:, halves[h]], in_=woven[:])
+            for b in range(2):
+                product(e, 2 + b, halves[h], scalar_bank(e, h)[:, halves[b]])
+
+        def vector_scatter(b, first, count, src):
+            nc.vector.tensor_copy(window[b][:].indirect(slots(first, count)), src)
+
+        def scalar_copy(e, h):
+            dx = held.tile([P, 2 * GROUP], F32, name=f"dx_scalar{e}{h}")
+            nc.scalar.copy(out=dx[:], in_=scalar_bank(e, h)[:])
+            return dx
+
+        def scalar_scatter(e, h, b, dx):
+            nc.scalar.activation(window[2 + b][:].indirect(slots(e * C + h * GROUP, GROUP)), dx[:, halves[b]], ACT.Copy)
+
+        last = PACK - 1
+        factor = [held.tile([P, C], F32, name=f"factor{d}") for d in range(last)]
+        factor.append(placed.tile([P, C], F32, name="factor_last", offset=8192 + 3072, align_bytes=64))
         for d in range(PACK):
             nc.vector.scalar_tensor_tensor(
-                out=factor[d][:, LATE:C].rearrange("p (n c) -> p n c", c=PACK),
-                in0=a0[d][:].rearrange("p (n c) -> p n c", c=PACK),
-                scalar=0.0, in1=gate0[:, LATE // PACK :, :], op0=ALU.is_gt, op1=ALU.mult,
+                out=factor[d][:].rearrange("p (n c) -> p n c", c=PACK), in0=a0[d][:].rearrange("p (n c) -> p n c", c=PACK),
+                scalar=0.0, in1=gate0, op0=ALU.is_gt, op1=ALU.mult,
             )
-        last_strand = PACK - 1
-        for d in range(last_strand):
-            gather(0, d, factor[d])
+        for d in range(last):
+            nc.vector.tensor_tensor(da0[:, d, :], dc[d][:].indirect(slots(0, C)), factor[d][:], ALU.mult)
+        for d in range(PACK):
+            nc.scalar.activation(picked[:, d, :], dc[d][:].indirect(slots(C, C)), ACT.Copy)
+        woven0 = [held.tile([P, GROUP * PACK], BF16, name=f"woven{h}", align_bytes=64) for h in range(2)]
         for h in range(2):
             nc.vector.tensor_tensor(
-                da[0][:, last_strand, half_slots[h]],
-                dc[last_strand][:].indirect(offsets[:, h * HALF // 16 : (h + 1) * HALF // 16]),
-                factor[last_strand][:, half_slots[h]], ALU.mult,
+                da0[:, last, halves[h]], dc[last][:].indirect(slots(h * GROUP, GROUP)), factor[last][:, halves[h]], ALU.mult
             )
-            if h == 0:
-                for first, stop in ((0, LATE), (LATE, HALF)):
-                    nc.scalar.copy(
-                        out=woven_by_four(woven[0][:, first * PACK : stop * PACK]),
-                        in_=strands_by_four(da[0][:, :, first:stop]),
-                    )
-            else:
-                weave_half(0, h)
-        nc.gpsimd.tensor_tensor(woven[0][:, 0 : LATE * PACK], woven[0][:, 0 : LATE * PACK], mask_late[:], ALU.mult)
-        sign_first = rows[:, 7 * C : 8 * C].bitcast(BF16)
-        sign_of(0, HALF, sign_first)
-        sign_third = rows[:, 6 * C : 6 * C + HALF].bitcast(BF16)
-        sign_of(HALF, P, sign_third)
-        quantize(0, woven[0][:])
+            if h == 1:
+                quantize(0, 0, woven0[0])
+            nc.vector.tensor_copy(out=woven_by_four(woven0[h][:]), in_=strands_by_four(da0[:, :, halves[h]]))
 
-        for d in range(2):
-            nc.vector.tensor_copy(ungated[:, d, :], dc[d][:].indirect(expert_list(1)))
-        for d in range(2, PACK):
-            gather(1, d, da[1][:, d - 2, :])
+        def factor1(h):
+            f = placed.tile([P, PACK, GROUP], F32, name=f"factor1{h}", offset=8192 + 4096 * h, align_bytes=64)
+            nc.vector.scalar_tensor_tensor(
+                out=f[:], in0=a1[:, :, halves[h]], scalar=0.0,
+                in1=gate1[:, halves[h]].unsqueeze(1).to_broadcast([P, PACK, GROUP]), op0=ALU.is_gt, op1=ALU.mult,
+            )
+            return f
+
+        def weave1(h, f, woven):
+            nc.gpsimd.tensor_tensor(woven_by_four(woven[:]), strands_by_four(picked[:, :, halves[h]]), strands_by_four(f[:]), ALU.mult)
+
+        factor_late = factor1(1)
+        quantize(0, 1, woven0[1])
+        for b in range(2):
+            product(0, b, slice(0, C), vector_bank(0, b)[:])
+        factor_early = factor1(0)
+        woven2 = placed.tile([P, GROUP * PACK], BF16, name="woven2", offset=1024, align_bytes=64)
+        weave1(0, factor_early, woven2)
+
         for h in range(2):
-            gated = da[1][:, 0:2, half_slots[h]]
-            nc.gpsimd.tensor_tensor(gated, ungated[:, :, half_slots[h]], gated, ALU.mult)
-        last_block = BLOCKS - 1
-        for b in range(BLOCKS):
-            product(0, b)
-        evacuate(0, 0)
-        mask = held.tile([P, C * PACK], BF16, name="mask", tag="codes0", align_bytes=64)
-        nc.scalar.activation(mask[:, half_woven[0]], sign_first, ACT.Relu)
-        evacuate(0, 1)
-        masked = held.tile([P, C * PACK], BF16, name="masked", align_bytes=64)
-        sign_fourth = held.tile([P, P * PACK], BF16, name="sign_fourth", tag="plane0", align_bytes=64)
-        sign_of(HALF + P, P, sign_fourth[:])
-        weave_half(1, 0)
-        nc.gpsimd.tensor_tensor(masked[:, half_woven[0]], woven[1][:, half_woven[0]], mask[:, half_woven[0]], ALU.mult)
-        nc.scalar.activation(mask[:, HALF * PACK : (HALF + P) * PACK], sign_third, ACT.Relu)
-        nc.scalar.activation(mask[:, (HALF + P) * PACK : C * PACK], sign_fourth[:], ACT.Relu)
-        weave_half(1, 1)
-        evacuate(0, 2)
-        nc.gpsimd.tensor_tensor(masked[:, half_woven[1]], woven[1][:, half_woven[1]], mask[:, half_woven[1]], ALU.mult)
-        evacuate(0, last_block, tag="codes0")
-        quantize(1, masked[:])
-        for b in range(BLOCKS):
-            product(1, b)
-            evacuate(1, b)
-
-        for e in range(E):
-            for b in range(BLOCKS):
-                scatter(e, b)
-        for b in range(BLOCKS):
+            dx = scalar_copy(0, h)
+            if h == 0:
+                dx00 = held.tile([P, C], F32, name="dx00")
+            for b in range(2):
+                scalar_scatter(0, h, b, dx)
+        nc.vector.tensor_copy(out=dx00[:], in_=vector_bank(0, 0)[:])
+        vector_scatter(0, 0, C, dx00[:])
+        quantize(1, 0, woven2)
+        product(1, 0, halves[0], vector_bank(1, 0)[:, halves[0]])
+        woven3 = placed.tile([P, GROUP * PACK], BF16, name="woven3", offset=2048, align_bytes=64)
+        weave1(1, factor_late, woven3)
+        dx01 = placed.tile([P, C], F32, name="dx01", offset=0, align_bytes=64)
+        nc.vector.tensor_copy(out=dx01[:], in_=vector_bank(0, 1)[:])
+        vector_scatter(1, 0, C, dx01[:])
+        dx_c = scalar_copy(1, 0)
+        scalar_scatter(1, 0, 0, dx_c)
+        quantize(1, 1, woven3)
+        dx10 = placed.tile([P, C], F32, name="dx10", offset=3072, align_bytes=64)
+        nc.vector.tensor_copy(out=dx10[:, halves[0]], in_=vector_bank(1, 0)[:, halves[0]])
+        vector_scatter(0, C, GROUP, dx10[:, halves[0]])
+        product(1, 0, halves[1], vector_bank(1, 0)[:, halves[1]])
+        product(1, 1, slice(0, C), vector_bank(1, 1)[:])
+        dx_d = scalar_copy(1, 1)
+        scalar_scatter(1, 1, 0, dx_d)
+        dx11 = held.tile([P, C], F32, name="dx11")
+        nc.scalar.copy(out=dx11[:], in_=vector_bank(1, 1)[:])
+        scalar_scatter(1, 0, 1, dx_c)
+        scalar_scatter(1, 1, 1, dx_d)
+        nc.vector.tensor_copy(out=dx10[:, halves[1]], in_=vector_bank(1, 0)[:, halves[1]])
+        vector_scatter(0, C + GROUP, GROUP, dx10[:, halves[1]])
+        vector_scatter(1, C, C, dx11[:])
+        for b in (2, 0, 3, 1):
             nc.sync.dma_start(out=out[b * P : (b + 1) * P, :], in_=window[b][:])

@@ -183,48 +183,50 @@ def tile_moe_sdb_relu_kernel(
             )
             return f
 
-        def weave1(h, f, woven):
-            nc.gpsimd.tensor_tensor(woven_by_four(woven[:]), strands_by_four(picked[:, :, halves[h]]), strands_by_four(f[:]), ALU.mult)
+        woven1 = [held.tile([P, GROUP * PACK], BF16, name=f"woven1{h}", align_bytes=64) for h in range(2)]
 
-        factor_late = factor1(1)
+        def weave1(h, f):
+            nc.vector.tensor_tensor(
+                woven_by_four(woven1[h][:]), strands_by_four(picked[:, :, halves[h]]), strands_by_four(f[:]), ALU.mult
+            )
+
+        def vector_block(e, b):
+            dx = held.tile([P, C], F32, name=f"dx_vector{e}{b}")
+            nc.scalar.copy(out=dx[:], in_=vector_bank(e, b)[:])
+            return dx
+
+        factors = [factor1(0)]
         quantize(0, 1, woven0[1])
         for b in range(2):
             product(0, b, slice(0, C), vector_bank(0, b)[:])
-        factor_early = factor1(0)
-        woven2 = placed.tile([P, GROUP * PACK], BF16, name="woven2", offset=1024, align_bytes=64)
-        weave1(0, factor_early, woven2)
-
+        factors.append(factor1(1))
         for h in range(2):
-            dx = scalar_copy(0, h)
-            if h == 0:
-                dx00 = held.tile([P, C], F32, name="dx00")
-            for b in range(2):
-                scalar_scatter(0, h, b, dx)
-        nc.vector.tensor_copy(out=dx00[:], in_=vector_bank(0, 0)[:])
+            weave1(h, factors[h])
+        for h in range(2):
+            quantize(1, h, woven1[h])
+        for b in range(2):
+            product(1, b, slice(0, C), vector_bank(1, b)[:])
+
+        dxs = {}
+        dxs[0, 0] = scalar_copy(0, 0)
+        scalar_scatter(0, 0, 0, dxs[0, 0])
+        scalar_scatter(0, 0, 1, dxs[0, 0])
+        dx00 = vector_block(0, 0)
+        dxs[0, 1] = scalar_copy(0, 1)
         vector_scatter(0, 0, C, dx00[:])
-        quantize(1, 0, woven2)
-        product(1, 0, halves[0], vector_bank(1, 0)[:, halves[0]])
-        woven3 = placed.tile([P, GROUP * PACK], BF16, name="woven3", offset=2048, align_bytes=64)
-        weave1(1, factor_late, woven3)
-        dx01 = placed.tile([P, C], F32, name="dx01", offset=0, align_bytes=64)
-        nc.vector.tensor_copy(out=dx01[:], in_=vector_bank(0, 1)[:])
+        scalar_scatter(0, 1, 0, dxs[0, 1])
+        dx10 = vector_block(1, 0)
+        vector_scatter(0, C, C, dx10[:])
+        scalar_scatter(0, 1, 1, dxs[0, 1])
+        dx01 = vector_block(0, 1)
         vector_scatter(1, 0, C, dx01[:])
-        dx_c = scalar_copy(1, 0)
-        scalar_scatter(1, 0, 0, dx_c)
-        quantize(1, 1, woven3)
-        dx10 = placed.tile([P, C], F32, name="dx10", offset=3072, align_bytes=64)
-        nc.vector.tensor_copy(out=dx10[:, halves[0]], in_=vector_bank(1, 0)[:, halves[0]])
-        vector_scatter(0, C, GROUP, dx10[:, halves[0]])
-        product(1, 0, halves[1], vector_bank(1, 0)[:, halves[1]])
-        product(1, 1, slice(0, C), vector_bank(1, 1)[:])
-        dx_d = scalar_copy(1, 1)
-        scalar_scatter(1, 1, 0, dx_d)
-        dx11 = held.tile([P, C], F32, name="dx11")
-        nc.scalar.copy(out=dx11[:], in_=vector_bank(1, 1)[:])
-        scalar_scatter(1, 0, 1, dx_c)
-        scalar_scatter(1, 1, 1, dx_d)
-        nc.vector.tensor_copy(out=dx10[:, halves[1]], in_=vector_bank(1, 0)[:, halves[1]])
-        vector_scatter(0, C + GROUP, GROUP, dx10[:, halves[1]])
+        for h in range(2):
+            dxs[1, h] = scalar_copy(1, h)
+        scalar_scatter(1, 0, 0, dxs[1, 0])
+        dx11 = vector_block(1, 1)
         vector_scatter(1, C, C, dx11[:])
-        for b in (2, 0, 3, 1):
+        scalar_scatter(1, 0, 1, dxs[1, 0])
+        scalar_scatter(1, 1, 0, dxs[1, 1])
+        scalar_scatter(1, 1, 1, dxs[1, 1])
+        for b in (0, 2, 3, 1):
             nc.sync.dma_start(out=out[b * P : (b + 1) * P, :], in_=window[b][:])

@@ -192,7 +192,10 @@ def tile_moe_sdb_relu_kernel(
 
         def vector_block(e, b):
             dx = held.tile([P, C], F32, name=f"dx_vector{e}{b}")
-            nc.scalar.copy(out=dx[:], in_=vector_bank(e, b)[:])
+            if b == 0:
+                nc.vector.tensor_copy(out=dx[:], in_=vector_bank(e, b)[:])
+            else:
+                nc.scalar.copy(out=dx[:], in_=vector_bank(e, b)[:])
             return dx
 
         factors = [factor1(0)]

@@ -7,7 +7,7 @@ K, T, E, C, H, N = 512, 1024, 2, 512, 512, 512
 P = 128
 PACK = 4
 GROUP = 256
-GROUPS = E * C // GROUP
+LENT = 128
 BLOCKS = K // P
 BANKS = 8
 FLOPS = 2 * N * H * T + 2 * H * K * E * C
@@ -43,11 +43,11 @@ def tile_moe_sdb_relu_kernel(
 
         offsets = held.tile([P, E * C // 16], U16, name="offsets")
         w2_raw = held.tile([P, H], I32, name="w2_raw", align_bytes=64)
-        w2_rows = held.tile([4, 4, H], U8, name="w2_rows", align_bytes=64)
+        w2_rows = held.tile([P, 2, H], U8, name="w2_rows", align_bytes=64)
         w2_zeroed = held.tile([P, H], U8, name="w2_zeroed", align_bytes=64)
         w2_codes = held.tile([P, H], I32, name="w2_codes", align_bytes=64)
         dy_codes = [held.tile([P, C], I32, name=f"dy_codes{h}", tag=f"dy{h}", align_bytes=64) for h in range(2)]
-        dy_rows = held.tile([P, 4, T], U8, name="dy_rows", align_bytes=64)
+        dy_rows = held.tile([P, 2, T], U8, name="dy_rows", align_bytes=64)
         dy_plane = dy_rows[:, 0, :]
         w1_codes = held.tile([P, E, K], I32, name="w1_codes", align_bytes=64)
         w1_plane = held.tile([P, E, K], U8, name="w1_plane", align_bytes=64)
@@ -62,16 +62,20 @@ def tile_moe_sdb_relu_kernel(
 
         a_rows = a.rearrange("(p d) s -> p d s", d=PACK)
         nc.sync.dma_start(out=gate_cols[:], in_=gate[0, 0:C].rearrange("(p c) -> p c", c=PACK))
-        nc.sync.dma_start(out=w2_rows[:].bitcast(I32), in_=w2t_scales[0].rearrange("(q r) i -> r q i", r=4).bitcast(I32))
-        nc.sync.dma_start(out=dy_rows[0:4].bitcast(I32), in_=dy_scales[0].rearrange("(q r) t -> r q t", r=4).bitcast(I32))
+        for rows, scales in ((w2_rows, w2t_scales), (dy_rows, dy_scales)):
+            for u in range(2):
+                nc.sync.dma_start(
+                    out=rows[64 * u : 64 * u + 4].bitcast(I32),
+                    in_=scales[0, 8 * u : 8 * u + 8].rearrange("(q r) i -> r q i", r=4).bitcast(I32),
+                )
         nc.sync.dma_start(out=w2_raw[:], in_=w2t_words[0].rearrange("p i d -> p (i d)").bitcast(I32))
         dy_flat = dy_words[0].rearrange("p t d -> p (t d)").bitcast(I32)
         for h in range(2):
             nc.sync.dma_start(out=dy_codes[h][:], in_=dy_flat[:, h * C : (h + 1) * C])
-        nc.sync.dma_start(out=a0[0][:], in_=a_rows[:, 0, 0:C])
-        nc.sync.dma_start(offsets[:], offs)
-        for d in range(1, PACK):
+        for d in range(PACK):
             nc.sync.dma_start(out=a0[d][:], in_=a_rows[:, d, 0:C])
+            if d == 1:
+                nc.sync.dma_start(offsets[:], offs)
         nc.sync.dma_start(out=w1_codes[:], in_=w1t_words[:, 0].rearrange("e p k d -> p e (k d)").bitcast(I32))
         for r in range(4):
             nc.sync.dma_start(
@@ -90,14 +94,16 @@ def tile_moe_sdb_relu_kernel(
         gate0 = gate_bank[:].rearrange("p (c n) -> p n c", c=PACK)
 
         for q in range(4):
-            nc.vector.tensor_copy(out=w2_zeroed[32 * q : 32 * q + 4, :].bitcast(I32), in_=w2_rows[:, q, :].bitcast(I32))
+            nc.vector.tensor_copy(out=w2_zeroed[32 * q : 32 * q + 4, :].bitcast(I32), in_=w2_rows[64 * (q // 2) : 64 * (q // 2) + 4, q % 2, :].bitcast(I32))
         w2_plane = held.tile([P, H], U8, name="w2_plane", tag="gate_cols", align_bytes=64)
         nc.vector.tensor_copy(
             out=w2_plane[:].rearrange("p (d c i) -> p c d i", d=PACK, i=16),
             in_=w2_zeroed[:].rearrange("p (c i d) -> p c d i", d=PACK, i=16),
         )
-        for q in range(1, 4):
-            nc.vector.tensor_copy(out=dy_plane[32 * q : 32 * q + 4, :].bitcast(I32), in_=dy_rows[0:4, q, :].bitcast(I32))
+        for u in range(2):
+            nc.vector.tensor_copy(
+                out=dy_plane[64 * u + 32 : 64 * u + 36, :].bitcast(I32), in_=dy_rows[64 * u : 64 * u + 4, 1, :].bitcast(I32)
+            )
         nc.scalar.copy(
             out=w2_codes[:].bitcast(U32).rearrange("p (d c i) -> p c d i", d=PACK, i=4),
             in_=w2_raw[:].bitcast(U32).rearrange("p (c i d) -> p c d i", d=PACK, i=4),
@@ -140,6 +146,8 @@ def tile_moe_sdb_relu_kernel(
 
         def quantize(e, h, woven):
             nc.vector.quantize_mx(out=codes[e][:, halves[h]].bitcast(E5M2), scales=plane[e][:, halves[h]], in_=woven[:])
+            if (e, h) == (0, 0):
+                product(0, 0, halves[0], vector_bank(0, 0)[:, halves[0]])
             for b in range(2):
                 product(e, 2 + b, halves[h], scalar_bank(e, h)[:, halves[b]])
 
@@ -157,12 +165,16 @@ def tile_moe_sdb_relu_kernel(
         last = PACK - 1
         factor = [held.tile([P, C], F32, name=f"factor{d}") for d in range(last)]
         factor.append(placed.tile([P, C], F32, name="factor_last", offset=8192 + 3072, align_bytes=64))
-        for d in range(PACK):
+
+        def factor0(d):
             nc.vector.scalar_tensor_tensor(
                 out=factor[d][:].rearrange("p (n c) -> p n c", c=PACK), in0=a0[d][:].rearrange("p (n c) -> p n c", c=PACK),
                 scalar=0.0, in1=gate0, op0=ALU.is_gt, op1=ALU.mult,
             )
+
+        factor0(0)
         for d in range(last):
+            factor0(d + 1)
             nc.vector.tensor_tensor(da0[:, d, :], dc[d][:].indirect(slots(0, C)), factor[d][:], ALU.mult)
         for d in range(PACK):
             nc.scalar.activation(picked[:, d, :], dc[d][:].indirect(slots(C, C)), ACT.Copy)
@@ -183,53 +195,53 @@ def tile_moe_sdb_relu_kernel(
             )
             return f
 
-        woven1 = [held.tile([P, GROUP * PACK], BF16, name=f"woven1{h}", align_bytes=64) for h in range(2)]
-
-        def weave1(h, f):
-            nc.vector.tensor_tensor(
-                woven_by_four(woven1[h][:]), strands_by_four(picked[:, :, halves[h]]), strands_by_four(f[:]), ALU.mult
+        def weave1(engine, h, f, woven):
+            engine.tensor_tensor(
+                woven_by_four(woven[:]), strands_by_four(picked[:, :, halves[h]]), strands_by_four(f[:]), ALU.mult
             )
 
-        def vector_block(e, b):
-            dx = held.tile([P, C], F32, name=f"dx_vector{e}{b}")
-            if b == 0:
-                nc.vector.tensor_copy(out=dx[:], in_=vector_bank(e, b)[:])
-            else:
-                nc.scalar.copy(out=dx[:], in_=vector_bank(e, b)[:])
-            return dx
-
-        factors = [factor1(0)]
+        factor_c = factor1(0)
+        dx00 = held.tile([P, C], F32, name="dx00")
+        nc.scalar.copy(out=dx00[:, halves[0]], in_=vector_bank(0, 0)[:, halves[0]])
+        dx_a = scalar_copy(0, 0)
         quantize(0, 1, woven0[1])
-        for b in range(2):
-            product(0, b, slice(0, C), vector_bank(0, b)[:])
-        factors.append(factor1(1))
-        for h in range(2):
-            weave1(h, factors[h])
-        for h in range(2):
-            quantize(1, h, woven1[h])
-        for b in range(2):
-            product(1, b, slice(0, C), vector_bank(1, b)[:])
+        product(0, 0, halves[1], vector_bank(0, 0)[:, halves[1]])
+        product(0, 1, slice(0, C), vector_bank(0, 1)[:])
+        woven_c = held.tile([P, GROUP * PACK], BF16, name="woven_c", tag="chain", align_bytes=64)
+        weave1(nc.vector, 0, factor_c, woven_c)
+        factor_d = factor1(1)
+        quantize(1, 0, woven_c)
+        product(1, 0, halves[0], vector_bank(1, 0)[:, halves[0]])
+        woven_d = held.tile([P, GROUP * PACK], BF16, name="woven_d", tag="chain", align_bytes=64)
+        weave1(nc.gpsimd, 1, factor_d, woven_d)
 
-        dxs = {}
-        dxs[0, 0] = scalar_copy(0, 0)
-        scalar_scatter(0, 0, 0, dxs[0, 0])
-        scalar_scatter(0, 0, 1, dxs[0, 0])
-        dx00 = vector_block(0, 0)
-        dxs[0, 1] = scalar_copy(0, 1)
-        vector_scatter(0, 0, C, dx00[:])
-        scalar_scatter(0, 1, 0, dxs[0, 1])
-        dx10 = vector_block(1, 0)
-        vector_scatter(0, C, C, dx10[:])
-        scalar_scatter(0, 1, 1, dxs[0, 1])
-        dx01 = vector_block(0, 1)
+        nc.scalar.activation(window[0][:].indirect(slots(0, LENT)), dx00[:, 0:LENT], ACT.Copy)
+        for b in range(2):
+            scalar_scatter(0, 0, b, dx_a)
+        nc.vector.tensor_copy(out=dx00[:, halves[1]], in_=vector_bank(0, 0)[:, halves[1]])
+        vector_scatter(0, LENT, C - LENT, dx00[:, LENT:C])
+        dx_b = scalar_copy(0, 1)
+        dx10 = [held.tile([P, GROUP], F32, name=f"dx10{h}") for h in range(2)]
+        nc.vector.tensor_copy(out=dx10[0][:], in_=vector_bank(1, 0)[:, halves[0]])
+        for b in range(2):
+            scalar_scatter(0, 1, b, dx_b)
+        vector_scatter(0, C, GROUP, dx10[0][:])
+        dx_c = scalar_copy(1, 0)
+        scalar_scatter(1, 0, 0, dx_c)
+        quantize(1, 1, woven_d)
+        product(1, 0, halves[1], vector_bank(1, 0)[:, halves[1]])
+        product(1, 1, slice(0, C), vector_bank(1, 1)[:])
+        dx01 = held.tile([P, C], F32, name="dx01", tag="chain", align_bytes=64)
+        nc.vector.tensor_copy(out=dx01[:], in_=vector_bank(0, 1)[:])
         vector_scatter(1, 0, C, dx01[:])
-        for h in range(2):
-            dxs[1, h] = scalar_copy(1, h)
-        scalar_scatter(1, 0, 0, dxs[1, 0])
-        dx11 = vector_block(1, 1)
+        dx_d = scalar_copy(1, 1)
+        dx11 = held.tile([P, C], F32, name="dx11")
+        nc.scalar.copy(out=dx11[:], in_=vector_bank(1, 1)[:])
+        scalar_scatter(1, 0, 1, dx_c)
+        for b in range(2):
+            scalar_scatter(1, 1, b, dx_d)
+        nc.vector.tensor_copy(out=dx10[1][:], in_=vector_bank(1, 0)[:, halves[1]])
+        vector_scatter(0, C + GROUP, GROUP, dx10[1][:])
         vector_scatter(1, C, C, dx11[:])
-        scalar_scatter(1, 0, 1, dxs[1, 0])
-        scalar_scatter(1, 1, 0, dxs[1, 1])
-        scalar_scatter(1, 1, 1, dxs[1, 1])
         for b in (0, 2, 3, 1):
             nc.sync.dma_start(out=out[b * P : (b + 1) * P, :], in_=window[b][:])

@@ -7,7 +7,6 @@ K, T, E, C, H, N = 512, 1024, 2, 512, 512, 512
 P = 128
 PACK = 4
 GROUP = 256
-LENT = 128
 BLOCKS = K // P
 BANKS = 8
 FLOPS = 2 * N * H * T + 2 * H * K * E * C
@@ -15,7 +14,6 @@ FLOPS = 2 * N * H * T + 2 * H * K * E * C
 F32 = mybir.dt.float32
 BF16 = mybir.dt.bfloat16
 I32 = mybir.dt.int32
-U32 = mybir.dt.uint32
 U16 = mybir.dt.uint16
 U8 = mybir.dt.uint8
 E4M3 = mybir.dt.float8_e4m3fn_x4
@@ -24,12 +22,12 @@ ALU = mybir.AluOpType
 ACT = mybir.ActivationFunctionType
 
 
-def strands_by_four(ap):
-    return ap.rearrange("p d (c i) -> p c d i", i=4)
+def strands_by_two(ap):
+    return ap.rearrange("p d (c i) -> p c d i", i=2)
 
 
-def woven_by_four(ap):
-    return ap.rearrange("p (c i d) -> p c d i", i=4, d=PACK)
+def woven_by_two(ap):
+    return ap.rearrange("p (c i d) -> p c d i", i=2, d=PACK)
 
 
 def tile_moe_sdb_relu_kernel(
@@ -45,7 +43,6 @@ def tile_moe_sdb_relu_kernel(
         w2_raw = held.tile([P, H], I32, name="w2_raw", align_bytes=64)
         w2_rows = held.tile([P, 2, H], U8, name="w2_rows", align_bytes=64)
         w2_zeroed = held.tile([P, H], U8, name="w2_zeroed", align_bytes=64)
-        w2_codes = held.tile([P, H], I32, name="w2_codes", align_bytes=64)
         dy_codes = [held.tile([P, C], I32, name=f"dy_codes{h}", tag=f"dy{h}", align_bytes=64) for h in range(2)]
         dy_rows = held.tile([P, 2, T], U8, name="dy_rows", align_bytes=64)
         dy_plane = dy_rows[:, 0, :]
@@ -61,13 +58,14 @@ def tile_moe_sdb_relu_kernel(
         nc.vector.memset(w2_zeroed[:].bitcast(I32), 0)
 
         a_rows = a.rearrange("(p d) s -> p d s", d=PACK)
-        nc.sync.dma_start(out=gate_cols[:], in_=gate[0, 0:C].rearrange("(p c) -> p c", c=PACK))
         for rows, scales in ((w2_rows, w2t_scales), (dy_rows, dy_scales)):
             for u in range(2):
                 nc.sync.dma_start(
                     out=rows[64 * u : 64 * u + 4].bitcast(I32),
                     in_=scales[0, 8 * u : 8 * u + 8].rearrange("(q r) i -> r q i", r=4).bitcast(I32),
                 )
+            if rows is w2_rows:
+                nc.sync.dma_start(out=gate_cols[:], in_=gate[0, 0:C].rearrange("(p c) -> p c", c=PACK))
         nc.sync.dma_start(out=w2_raw[:], in_=w2t_words[0].rearrange("p i d -> p (i d)").bitcast(I32))
         dy_flat = dy_words[0].rearrange("p t d -> p (t d)").bitcast(I32)
         for h in range(2):
@@ -95,7 +93,8 @@ def tile_moe_sdb_relu_kernel(
 
         for q in range(4):
             nc.vector.tensor_copy(out=w2_zeroed[32 * q : 32 * q + 4, :].bitcast(I32), in_=w2_rows[64 * (q // 2) : 64 * (q // 2) + 4, q % 2, :].bitcast(I32))
-        w2_plane = held.tile([P, H], U8, name="w2_plane", tag="gate_cols", align_bytes=64)
+        w2_codes = held.tile([P, H], I32, name="w2_codes", tag="gate_cols", align_bytes=64)
+        w2_plane = held.tile([P, H], U8, name="w2_plane", align_bytes=64)
         nc.vector.tensor_copy(
             out=w2_plane[:].rearrange("p (d c i) -> p c d i", d=PACK, i=16),
             in_=w2_zeroed[:].rearrange("p (c i d) -> p c d i", d=PACK, i=16),
@@ -104,9 +103,9 @@ def tile_moe_sdb_relu_kernel(
             nc.vector.tensor_copy(
                 out=dy_plane[64 * u + 32 : 64 * u + 36, :].bitcast(I32), in_=dy_rows[64 * u : 64 * u + 4, 1, :].bitcast(I32)
             )
-        nc.scalar.copy(
-            out=w2_codes[:].bitcast(U32).rearrange("p (d c i) -> p c d i", d=PACK, i=4),
-            in_=w2_raw[:].bitcast(U32).rearrange("p (c i d) -> p c d i", d=PACK, i=4),
+        nc.vector.tensor_copy(
+            out=w2_codes[:].rearrange("p (d c i) -> p c d i", d=PACK, i=4),
+            in_=w2_raw[:].rearrange("p (c i d) -> p c d i", d=PACK, i=4),
         )
 
         dc = [held.tile([P, T], F32, name=f"dc{d}") for d in range(PACK)]
@@ -124,7 +123,7 @@ def tile_moe_sdb_relu_kernel(
         def slots(first, count):
             return offsets[:, first // 16 : (first + count) // 16]
 
-        window = [held.tile([P, T], F32, name=f"window{b}") for b in range(BLOCKS)]
+        window = {b: held.tile([P, T], F32, name=f"window{b}") for b in (0, 2, 3)}
         codes = [held.tile([P, C], I32, name=f"codes{e}", align_bytes=64) for e in range(E)]
         plane = [held.tile([P, C], U8, name=f"plane{e}", align_bytes=64) for e in range(E)]
         da0 = held.tile([P, PACK, C], F32, name="da0")
@@ -138,33 +137,20 @@ def tile_moe_sdb_relu_kernel(
                 rhs=codes[e][:, cols].bitcast(E5M2), rhs_scale=plane[e][:, cols], start=True, stop=True,
             )
 
-        def vector_bank(e, b):
-            return banks[4 * e + b]
-
-        def scalar_bank(e, h):
-            return banks[4 * e + 2 + h]
-
         def quantize(e, h, woven):
             nc.vector.quantize_mx(out=codes[e][:, halves[h]].bitcast(E5M2), scales=plane[e][:, halves[h]], in_=woven[:])
-            if (e, h) == (0, 0):
-                product(0, 0, halves[0], vector_bank(0, 0)[:, halves[0]])
-            for b in range(2):
-                product(e, 2 + b, halves[h], scalar_bank(e, h)[:, halves[b]])
 
         def vector_scatter(b, first, count, src):
             nc.vector.tensor_copy(window[b][:].indirect(slots(first, count)), src)
 
-        def scalar_copy(e, h):
-            dx = held.tile([P, 2 * GROUP], F32, name=f"dx_scalar{e}{h}")
-            nc.scalar.copy(out=dx[:], in_=scalar_bank(e, h)[:])
-            return dx
+        def scalar_scatter(b, first, src):
+            nc.scalar.activation(window[b][:].indirect(slots(first, GROUP)), src, ACT.Copy)
 
-        def scalar_scatter(e, h, b, dx):
-            nc.scalar.activation(window[2 + b][:].indirect(slots(e * C + h * GROUP, GROUP)), dx[:, halves[b]], ACT.Copy)
+        whole = slice(0, C)
 
         last = PACK - 1
         factor = [held.tile([P, C], F32, name=f"factor{d}") for d in range(last)]
-        factor.append(placed.tile([P, C], F32, name="factor_last", offset=8192 + 3072, align_bytes=64))
+        factor.append(placed.tile([P, C], F32, name="factor_last", offset=12288 + 3072, align_bytes=64))
 
         def factor0(d):
             nc.vector.scalar_tensor_tensor(
@@ -185,63 +171,84 @@ def tile_moe_sdb_relu_kernel(
             )
             if h == 1:
                 quantize(0, 0, woven0[0])
-            nc.vector.tensor_copy(out=woven_by_four(woven0[h][:]), in_=strands_by_four(da0[:, :, halves[h]]))
+                for b in range(2):
+                    product(0, 2 + b, halves[0], banks[2][:, halves[b]])
+            nc.vector.tensor_copy(out=woven_by_two(woven0[h][:]), in_=strands_by_two(da0[:, :, halves[h]]))
 
-        def factor1(h):
-            f = placed.tile([P, PACK, GROUP], F32, name=f"factor1{h}", offset=8192 + 4096 * h, align_bytes=64)
+        factor1 = [
+            placed.tile([P, PACK, GROUP], F32, name=f"factor1{h}", offset=12288 + 4096 * h, align_bytes=64) for h in range(2)
+        ]
+
+        def factor1_pair(h, u):
+            pair = slice(2 * u, 2 * u + 2)
             nc.vector.scalar_tensor_tensor(
-                out=f[:], in0=a1[:, :, halves[h]], scalar=0.0,
-                in1=gate1[:, halves[h]].unsqueeze(1).to_broadcast([P, PACK, GROUP]), op0=ALU.is_gt, op1=ALU.mult,
-            )
-            return f
-
-        def weave1(engine, h, f, woven):
-            engine.tensor_tensor(
-                woven_by_four(woven[:]), strands_by_four(picked[:, :, halves[h]]), strands_by_four(f[:]), ALU.mult
+                out=factor1[h][:, pair, :], in0=a1[:, pair, halves[h]], scalar=0.0,
+                in1=gate1[:, halves[h]].unsqueeze(1).to_broadcast([P, 2, GROUP]), op0=ALU.is_gt, op1=ALU.mult,
             )
 
-        factor_c = factor1(0)
-        dx00 = held.tile([P, C], F32, name="dx00")
-        nc.scalar.copy(out=dx00[:, halves[0]], in_=vector_bank(0, 0)[:, halves[0]])
-        dx_a = scalar_copy(0, 0)
+        def weave1(h, f, woven):
+            nc.gpsimd.tensor_tensor(
+                woven_by_two(woven[:]), strands_by_two(picked[:, :, halves[h]]), strands_by_two(f[:]), ALU.mult
+            )
+
+        def staged(name, pool=held, **where):
+            return pool.tile([P, C], F32, name=name, **where)
+
+        def scalar_group(first, bank):
+            dx = staged(f"dx_scalar{first}")
+            for b in range(2):
+                nc.scalar.copy(out=dx[:, halves[b]], in_=bank[:, halves[b]])
+            return dx
+
+        factor1_pair(1, 0)
+        dx_a = scalar_group(0, banks[2])
         quantize(0, 1, woven0[1])
-        product(0, 0, halves[1], vector_bank(0, 0)[:, halves[1]])
-        product(0, 1, slice(0, C), vector_bank(0, 1)[:])
-        woven_c = held.tile([P, GROUP * PACK], BF16, name="woven_c", tag="chain", align_bytes=64)
-        weave1(nc.vector, 0, factor_c, woven_c)
-        factor_d = factor1(1)
-        quantize(1, 0, woven_c)
-        product(1, 0, halves[0], vector_bank(1, 0)[:, halves[0]])
-        woven_d = held.tile([P, GROUP * PACK], BF16, name="woven_d", tag="chain", align_bytes=64)
-        weave1(nc.gpsimd, 1, factor_d, woven_d)
+        product(0, 0, whole, banks[0][:])
+        for b in range(2):
+            product(0, 2 + b, halves[1], banks[3][:, halves[b]])
+        product(0, 1, whole, banks[1][:])
+        factor1_pair(1, 1)
+        factor1_pair(0, 0)
+        dx0 = [staged(f"dx0{b}") for b in range(2)]
+        nc.vector.tensor_copy(out=dx0[0][:], in_=banks[0][:])
+        factor1_pair(0, 1)
+        woven_c = held.tile([P, GROUP * PACK], BF16, name="woven_c", tag="woven1", align_bytes=64)
+        weave1(0, factor1[0], woven_c)
 
-        nc.scalar.activation(window[0][:].indirect(slots(0, LENT)), dx00[:, 0:LENT], ACT.Copy)
         for b in range(2):
-            scalar_scatter(0, 0, b, dx_a)
-        nc.vector.tensor_copy(out=dx00[:, halves[1]], in_=vector_bank(0, 0)[:, halves[1]])
-        vector_scatter(0, LENT, C - LENT, dx00[:, LENT:C])
-        dx_b = scalar_copy(0, 1)
-        dx10 = [held.tile([P, GROUP], F32, name=f"dx10{h}") for h in range(2)]
-        nc.vector.tensor_copy(out=dx10[0][:], in_=vector_bank(1, 0)[:, halves[0]])
+            scalar_scatter(2 + b, 0, dx_a[:, halves[b]])
+        vector_scatter(0, 0, C, dx0[0][:])
+        dx_b = scalar_group(GROUP, banks[3])
+        nc.scalar.copy(out=dx0[1][:], in_=banks[1][:])
         for b in range(2):
-            scalar_scatter(0, 1, b, dx_b)
-        vector_scatter(0, C, GROUP, dx10[0][:])
-        dx_c = scalar_copy(1, 0)
-        scalar_scatter(1, 0, 0, dx_c)
+            scalar_scatter(2 + b, GROUP, dx_b[:, halves[b]])
+        quantize(1, 0, woven_c)
+        product(1, 0, halves[0], banks[4][:, halves[0]])
+        for b in range(2):
+            product(1, 2 + b, halves[0], banks[6][:, halves[b]])
+        product(1, 1, halves[0], banks[5][:, halves[0]])
+        woven_d = held.tile([P, GROUP * PACK], BF16, name="woven_d", tag="woven1", align_bytes=64)
+        weave1(1, factor1[1], woven_d)
+        window[1] = placed.tile([P, T], F32, name="window1", offset=12288 - 2048, align_bytes=64)
+        vector_scatter(1, 0, C, dx0[1][:])
+
+        dx_c = scalar_group(C, banks[6])
+        for b in range(2):
+            scalar_scatter(2 + b, C, dx_c[:, halves[b]])
         quantize(1, 1, woven_d)
-        product(1, 0, halves[1], vector_bank(1, 0)[:, halves[1]])
-        product(1, 1, slice(0, C), vector_bank(1, 1)[:])
-        dx01 = held.tile([P, C], F32, name="dx01", tag="chain", align_bytes=64)
-        nc.vector.tensor_copy(out=dx01[:], in_=vector_bank(0, 1)[:])
-        vector_scatter(1, 0, C, dx01[:])
-        dx_d = scalar_copy(1, 1)
-        dx11 = held.tile([P, C], F32, name="dx11")
-        nc.scalar.copy(out=dx11[:], in_=vector_bank(1, 1)[:])
-        scalar_scatter(1, 0, 1, dx_c)
+        for b in range(BLOCKS):
+            product(1, b, halves[1], banks[(0, 1, 7, 7)[b]][:, halves[b // 3]])
+        dx1 = placed.tile([P, 2, C], F32, name="dx1", offset=12288 + 4096 + 2048, align_bytes=64)
+        dx10, dx11 = dx1[:, 0, :], dx1[:, 1, :]
+        nc.vector.tensor_copy(out=dx10[:, halves[0]], in_=banks[4][:, halves[0]])
+        nc.vector.tensor_copy(out=dx11[:, halves[0]], in_=banks[5][:, halves[0]])
+        vector_scatter(0, C, GROUP, dx10[:, halves[0]])
+        nc.vector.tensor_copy(out=dx10[:, halves[1]], in_=banks[0][:, halves[0]])
+        nc.vector.tensor_copy(out=dx11[:, halves[1]], in_=banks[1][:, halves[0]])
+        dx_d = scalar_group(C + GROUP, banks[7])
         for b in range(2):
-            scalar_scatter(1, 1, b, dx_d)
-        nc.vector.tensor_copy(out=dx10[1][:], in_=vector_bank(1, 0)[:, halves[1]])
-        vector_scatter(0, C + GROUP, GROUP, dx10[1][:])
-        vector_scatter(1, C, C, dx11[:])
+            scalar_scatter(2 + b, C + GROUP, dx_d[:, halves[b]])
+        vector_scatter(0, C + GROUP, GROUP, dx10[:, halves[1]])
+        vector_scatter(1, C, C, dx11)
         for b in (0, 2, 3, 1):
             nc.sync.dma_start(out=out[b * P : (b + 1) * P, :], in_=window[b][:])

@@ -9,6 +9,7 @@ PACK = 4
 GROUP = 256
 BLOCKS = K // P
 BANKS = 8
+LATE = 32
 FLOPS = 2 * N * H * T + 2 * H * K * E * C
 
 F32 = mybir.dt.float32
@@ -49,11 +50,13 @@ def tile_moe_sdb_relu_kernel(
         w1_codes = held.tile([P, E, K], I32, name="w1_codes", align_bytes=64)
         w1_plane = held.tile([P, E, K], U8, name="w1_plane", align_bytes=64)
         gate_cols = held.tile([P, PACK], F32, name="gate_cols", tag="gate_cols", align_bytes=64)
-        gate1 = held.tile([P, C], F32, name="gate1")
+        gate1_cols = held.tile([P, PACK], F32, name="gate1_cols")
         identity = held.tile([P, P], F32, name="identity")
         banks = [psum.tile([P, C], F32, name=f"bank{b}") for b in range(BANKS)]
         a0 = [held.tile([P, C], F32, name=f"a0{d}") for d in range(PACK)]
-        a1 = held.tile([P, PACK, C], F32, name="a1")
+        shared = placed.tile([P, 2 * PACK * C - GROUP], F32, name="shared", offset=0)
+        da0 = shared[:, 0 : PACK * C].rearrange("p (d s) -> p d s", d=PACK)
+        a1 = shared[:, PACK * C - GROUP :].rearrange("p (d s) -> p d s", d=PACK)
 
         nc.vector.memset(w2_zeroed[:].bitcast(I32), 0)
 
@@ -74,14 +77,14 @@ def tile_moe_sdb_relu_kernel(
             nc.sync.dma_start(out=a0[d][:], in_=a_rows[:, d, 0:C])
             if d == 1:
                 nc.sync.dma_start(offsets[:], offs)
+        nc.sync.dma_start(out=gate1_cols[:], in_=gate[0, C : 2 * C].rearrange("(p c) -> p c", c=PACK))
         nc.sync.dma_start(out=w1_codes[:], in_=w1t_words[:, 0].rearrange("e p k d -> p e (k d)").bitcast(I32))
         for r in range(4):
             nc.sync.dma_start(
                 out=w1_plane[r:P:32, :, :].bitcast(I32),
                 in_=w1t_scales[:, 0, r:16:4, :].rearrange("e q k -> q e k").bitcast(I32),
             )
-        nc.sync.dma_start(out=a1[:], in_=a_rows[:, :, C : 2 * C])
-        nc.sync.dma_start(out=gate1[:], in_=gate[:, C : 2 * C])
+        nc.sync.dma_start(out=a1, in_=a_rows[:, :, C : 2 * C])
 
         make_identity(nc, identity[:])
         gate_bank = banks[BANKS - 1]
@@ -120,135 +123,126 @@ def tile_moe_sdb_relu_kernel(
                 )
                 nc.scalar.copy(out=dc[d][:, toks], in_=bank[:])
 
+        gate1 = banks[0]
+        for c in range(PACK):
+            nc.tensor.transpose(gate1[:, c:C:PACK], gate1_cols[:, c : c + 1].to_broadcast([P, P]), identity[:])
+
         def slots(first, count):
             return offsets[:, first // 16 : (first + count) // 16]
 
-        window = {b: held.tile([P, T], F32, name=f"window{b}") for b in (0, 2, 3)}
-        codes = [held.tile([P, C], I32, name=f"codes{e}", align_bytes=64) for e in range(E)]
-        plane = [held.tile([P, C], U8, name=f"plane{e}", align_bytes=64) for e in range(E)]
-        da0 = held.tile([P, PACK, C], F32, name="da0")
-        picked = held.tile([P, PACK, C], F32, name="picked", tag="dy1", align_bytes=64)
+        window = {b: held.tile([P, T], F32, name=f"window{b}") for b in (2, 3)}
+        codes = held.tile([P, GROUP], I32, name="codes", align_bytes=64)
+        plane = held.tile([P, GROUP], U8, name="plane", align_bytes=64)
+        early = GROUP - LATE
+        shared1 = held.tile([P, 2, early + PACK * C], F32, name="shared1", tag="dy1", align_bytes=64)
+        factor1 = shared1[:, 0, early:].rearrange("p (h d s) -> p h d s", h=2, d=PACK)
+        picked = shared1[:, 1, early:].rearrange("p (d s) -> p d s", d=PACK)
         halves = [slice(0, GROUP), slice(GROUP, C)]
 
-        def product(e, b, cols, dst):
-            rows = slice(b * P, (b + 1) * P)
-            nc.tensor.matmul_mx(
-                out=dst, lhsT=w1_codes[:, e, rows].bitcast(E4M3), lhsT_scale=w1_plane[:, e, rows],
-                rhs=codes[e][:, cols].bitcast(E5M2), rhs_scale=plane[e][:, cols], start=True, stop=True,
-            )
+        def result(g, b):
+            if g == 1:
+                return banks[4 + b // 2][:, halves[b % 2]]
+            return banks[((1, 2, 3), (), (7, 6, 1), (2, 3, 4))[g][(1, 2, 0, 0)[b]]][:, halves[b // 3]]
 
-        def quantize(e, h, woven):
-            nc.vector.quantize_mx(out=codes[e][:, halves[h]].bitcast(E5M2), scales=plane[e][:, halves[h]], in_=woven[:])
+        def quantize_and_multiply(g, woven):
+            nc.vector.quantize_mx(out=codes[:].bitcast(E5M2), scales=plane[:], in_=woven[:])
+            for b in (2, 3, 0, 1):
+                rows = slice(b * P, (b + 1) * P)
+                nc.tensor.matmul_mx(
+                    out=result(g, b), lhsT=w1_codes[:, g // 2, rows].bitcast(E4M3), lhsT_scale=w1_plane[:, g // 2, rows],
+                    rhs=codes[:].bitcast(E5M2), rhs_scale=plane[:], start=True, stop=True,
+                )
 
         def vector_scatter(b, first, count, src):
             nc.vector.tensor_copy(window[b][:].indirect(slots(first, count)), src)
 
-        def scalar_scatter(b, first, src):
-            nc.scalar.activation(window[b][:].indirect(slots(first, GROUP)), src, ACT.Copy)
+        def vector_copies(g, staged):
+            for b in range(2):
+                nc.vector.tensor_copy(out=staged[b], in_=result(g, b))
 
-        whole = slice(0, C)
+        def scalar_group(g):
+            dx = held.tile([P, C], F32, name=f"dx_scalar{g}")
+            for b in range(2):
+                nc.scalar.copy(out=dx[:, halves[b]], in_=result(g, 2 + b))
+            for b in range(2):
+                nc.scalar.activation(window[2 + b][:].indirect(slots(g * GROUP, GROUP)), dx[:, halves[b]], ACT.Copy)
+
+        def woven_tile(g):
+            return held.tile([P, GROUP * PACK], BF16, name=f"woven{g}", tag="woven", align_bytes=64)
+
+        def weave0(h):
+            woven = woven_tile(h)
+            nc.gpsimd.tensor_scalar(
+                woven[:].rearrange("p (s d) -> p s d", d=PACK), da0[:, :, halves[h]].rearrange("p d s -> p s d"),
+                1.0, 0.0, ALU.mult, ALU.add,
+            )
+            return woven
+
+        def weave1(h):
+            woven = woven_tile(2 + h)
+            nc.gpsimd.tensor_tensor(
+                woven_by_two(woven[:]), strands_by_two(picked[:, :, halves[h]]), strands_by_two(factor1[:, h]),
+                ALU.mult,
+            )
+            return woven
+
+        def factor(dst, saved, gate_rows):
+            nc.vector.scalar_tensor_tensor(out=dst, in0=saved, scalar=0.0, in1=gate_rows, op0=ALU.is_gt, op1=ALU.mult)
+
+        def by_fours(ap):
+            return ap.rearrange("p (n c) -> p n c", c=PACK)
+
+        def by_halves(ap):
+            return ap.rearrange("p (h s) -> p h s", h=2)
 
         last = PACK - 1
-        factor = [held.tile([P, C], F32, name=f"factor{d}") for d in range(last)]
-        factor.append(placed.tile([P, C], F32, name="factor_last", offset=12288 + 3072, align_bytes=64))
+        factor0 = [held.tile([P, C], F32, name=f"factor0{d}") for d in range(PACK)]
 
-        def factor0(d):
-            nc.vector.scalar_tensor_tensor(
-                out=factor[d][:].rearrange("p (n c) -> p n c", c=PACK), in0=a0[d][:].rearrange("p (n c) -> p n c", c=PACK),
-                scalar=0.0, in1=gate0, op0=ALU.is_gt, op1=ALU.mult,
-            )
-
-        factor0(0)
+        factor(by_fours(factor0[0][:]), by_fours(a0[0][:]), gate0)
         for d in range(last):
-            factor0(d + 1)
-            nc.vector.tensor_tensor(da0[:, d, :], dc[d][:].indirect(slots(0, C)), factor[d][:], ALU.mult)
+            factor(by_fours(factor0[d + 1][:]), by_fours(a0[d + 1][:]), gate0)
+            nc.vector.tensor_tensor(da0[:, d, :], dc[d][:].indirect(slots(0, C)), factor0[d][:], ALU.mult)
         for d in range(PACK):
             nc.scalar.activation(picked[:, d, :], dc[d][:].indirect(slots(C, C)), ACT.Copy)
-        woven0 = [held.tile([P, GROUP * PACK], BF16, name=f"woven{h}", align_bytes=64) for h in range(2)]
-        for h in range(2):
+
+        def last_gather(h):
             nc.vector.tensor_tensor(
-                da0[:, last, halves[h]], dc[last][:].indirect(slots(h * GROUP, GROUP)), factor[last][:, halves[h]], ALU.mult
-            )
-            if h == 1:
-                quantize(0, 0, woven0[0])
-                for b in range(2):
-                    product(0, 2 + b, halves[0], banks[2][:, halves[b]])
-            nc.vector.tensor_copy(out=woven_by_two(woven0[h][:]), in_=strands_by_two(da0[:, :, halves[h]]))
-
-        factor1 = [
-            placed.tile([P, PACK, GROUP], F32, name=f"factor1{h}", offset=12288 + 4096 * h, align_bytes=64) for h in range(2)
-        ]
-
-        def factor1_pair(h, u):
-            pair = slice(2 * u, 2 * u + 2)
-            nc.vector.scalar_tensor_tensor(
-                out=factor1[h][:, pair, :], in0=a1[:, pair, halves[h]], scalar=0.0,
-                in1=gate1[:, halves[h]].unsqueeze(1).to_broadcast([P, 2, GROUP]), op0=ALU.is_gt, op1=ALU.mult,
+                da0[:, last, halves[h]], dc[last][:].indirect(slots(h * GROUP, GROUP)), factor0[last][:, halves[h]], ALU.mult
             )
 
-        def weave1(h, f, woven):
-            nc.gpsimd.tensor_tensor(
-                woven_by_two(woven[:]), strands_by_two(picked[:, :, halves[h]]), strands_by_two(f[:]), ALU.mult
-            )
-
-        def staged(name, pool=held, **where):
-            return pool.tile([P, C], F32, name=name, **where)
-
-        def scalar_group(first, bank):
-            dx = staged(f"dx_scalar{first}")
-            for b in range(2):
-                nc.scalar.copy(out=dx[:, halves[b]], in_=bank[:, halves[b]])
-            return dx
-
-        factor1_pair(1, 0)
-        dx_a = scalar_group(0, banks[2])
-        quantize(0, 1, woven0[1])
-        product(0, 0, whole, banks[0][:])
+        last_gather(0)
+        woven = weave0(0)
+        for d in range(last):
+            factor(factor1[:, :, d, :], by_halves(a1[:, d, :]), by_halves(gate1[:]))
+        quantize_and_multiply(0, woven)
+        last_gather(1)
+        woven = weave0(1)
+        factor(factor1[:, :, last, :], by_halves(a1[:, last, :]), by_halves(gate1[:]))
+        scalar_group(0)
+        dx_a = held.tile([P, 2, GROUP], F32, name="dx_a")
+        vector_copies(0, [dx_a[:, b, :] for b in range(2)])
+        quantize_and_multiply(1, woven)
+        woven = weave1(0)
         for b in range(2):
-            product(0, 2 + b, halves[1], banks[3][:, halves[b]])
-        product(0, 1, whole, banks[1][:])
-        factor1_pair(1, 1)
-        factor1_pair(0, 0)
-        dx0 = [staged(f"dx0{b}") for b in range(2)]
-        nc.vector.tensor_copy(out=dx0[0][:], in_=banks[0][:])
-        factor1_pair(0, 1)
-        woven_c = held.tile([P, GROUP * PACK], BF16, name="woven_c", tag="woven1", align_bytes=64)
-        weave1(0, factor1[0], woven_c)
-
+            window[b] = placed.tile([P, T], F32, name=f"window{b}", offset=4 * T * b)
+            vector_scatter(b, 0, GROUP, dx_a[:, b, :])
+        scalar_group(1)
+        for cols in (slice(0, early), slice(early, GROUP)):
+            nc.vector.tensor_copy(out=shared1[:, :, cols], in_=by_halves(banks[4][:])[:, :, cols])
+        quantize_and_multiply(2, woven)
+        woven = weave1(1)
         for b in range(2):
-            scalar_scatter(2 + b, 0, dx_a[:, halves[b]])
-        vector_scatter(0, 0, C, dx0[0][:])
-        dx_b = scalar_group(GROUP, banks[3])
-        nc.scalar.copy(out=dx0[1][:], in_=banks[1][:])
-        for b in range(2):
-            scalar_scatter(2 + b, GROUP, dx_b[:, halves[b]])
-        quantize(1, 0, woven_c)
-        product(1, 0, halves[0], banks[4][:, halves[0]])
-        for b in range(2):
-            product(1, 2 + b, halves[0], banks[6][:, halves[b]])
-        product(1, 1, halves[0], banks[5][:, halves[0]])
-        woven_d = held.tile([P, GROUP * PACK], BF16, name="woven_d", tag="woven1", align_bytes=64)
-        weave1(1, factor1[1], woven_d)
-        window[1] = placed.tile([P, T], F32, name="window1", offset=12288 - 2048, align_bytes=64)
-        vector_scatter(1, 0, C, dx0[1][:])
-
-        dx_c = scalar_group(C, banks[6])
-        for b in range(2):
-            scalar_scatter(2 + b, C, dx_c[:, halves[b]])
-        quantize(1, 1, woven_d)
-        for b in range(BLOCKS):
-            product(1, b, halves[1], banks[(0, 1, 7, 7)[b]][:, halves[b // 3]])
-        dx1 = placed.tile([P, 2, C], F32, name="dx1", offset=12288 + 4096 + 2048, align_bytes=64)
-        dx10, dx11 = dx1[:, 0, :], dx1[:, 1, :]
-        nc.vector.tensor_copy(out=dx10[:, halves[0]], in_=banks[4][:, halves[0]])
-        nc.vector.tensor_copy(out=dx11[:, halves[0]], in_=banks[5][:, halves[0]])
-        vector_scatter(0, C, GROUP, dx10[:, halves[0]])
-        nc.vector.tensor_copy(out=dx10[:, halves[1]], in_=banks[0][:, halves[0]])
-        nc.vector.tensor_copy(out=dx11[:, halves[1]], in_=banks[1][:, halves[0]])
-        dx_d = scalar_group(C + GROUP, banks[7])
-        for b in range(2):
-            scalar_scatter(2 + b, C + GROUP, dx_d[:, halves[b]])
-        vector_scatter(0, C + GROUP, GROUP, dx10[:, halves[1]])
-        vector_scatter(1, C, C, dx11)
+            vector_scatter(b, GROUP, GROUP, shared1[:, b, 0:GROUP])
+        scalar_group(2)
+        dx1 = held.tile([P, C], F32, name="dx1")
+        dx_c = factor1[:, 1, 0, :]
+        dx_d = held.tile([P, GROUP], F32, name="dx_d")
+        vector_copies(2, [dx_c, dx1[:, halves[0]]])
+        quantize_and_multiply(3, woven)
+        vector_scatter(0, C, GROUP, dx_c)
+        scalar_group(3)
+        vector_copies(3, [dx_d[:], dx1[:, halves[1]]])
+        vector_scatter(0, C + GROUP, GROUP, dx_d[:])
+        vector_scatter(1, C, C, dx1[:])
         for b in (0, 2, 3, 1):
             nc.sync.dma_start(out=out[b * P : (b + 1) * P, :], in_=window[b][:])

@@ -9,7 +9,6 @@ PACK = 4
 GROUP = 256
 BLOCKS = K // P
 BANKS = 8
-LATE = 32
 FLOPS = 2 * N * H * T + 2 * H * K * E * C
 
 F32 = mybir.dt.float32
@@ -37,7 +36,6 @@ def tile_moe_sdb_relu_kernel(
     nc = tc.nc
     with ExitStack() as ctx:
         held = ctx.enter_context(tc.tile_pool(name="held", bufs=1))
-        placed = ctx.enter_context(tc.tile_pool(name="placed", bufs=1))
         psum = ctx.enter_context(tc.psum_pool(name="psum", bufs=1))
 
         offsets = held.tile([P, E * C // 16], U16, name="offsets")
@@ -54,9 +52,7 @@ def tile_moe_sdb_relu_kernel(
         identity = held.tile([P, P], F32, name="identity")
         banks = [psum.tile([P, C], F32, name=f"bank{b}") for b in range(BANKS)]
         a0 = [held.tile([P, C], F32, name=f"a0{d}") for d in range(PACK)]
-        shared = placed.tile([P, 2 * PACK * C - GROUP], F32, name="shared", offset=0)
-        da0 = shared[:, 0 : PACK * C].rearrange("p (d s) -> p d s", d=PACK)
-        a1 = shared[:, PACK * C - GROUP :].rearrange("p (d s) -> p d s", d=PACK)
+        a1 = held.tile([P, PACK, C], F32, name="a1")
 
         nc.vector.memset(w2_zeroed[:].bitcast(I32), 0)
 
@@ -84,7 +80,7 @@ def tile_moe_sdb_relu_kernel(
                 out=w1_plane[r:P:32, :, :].bitcast(I32),
                 in_=w1t_scales[:, 0, r:16:4, :].rearrange("e q k -> q e k").bitcast(I32),
             )
-        nc.sync.dma_start(out=a1, in_=a_rows[:, :, C : 2 * C])
+        nc.sync.dma_start(out=a1[:], in_=a_rows[:, :, C : 2 * C])
 
         make_identity(nc, identity[:])
         gate_bank = banks[BANKS - 1]
@@ -130,35 +126,37 @@ def tile_moe_sdb_relu_kernel(
         def slots(first, count):
             return offsets[:, first // 16 : (first + count) // 16]
 
-        window = {b: held.tile([P, T], F32, name=f"window{b}") for b in (2, 3)}
-        codes = held.tile([P, GROUP], I32, name="codes", align_bytes=64)
-        plane = held.tile([P, GROUP], U8, name="plane", align_bytes=64)
-        early = GROUP - LATE
-        shared1 = held.tile([P, 2, early + PACK * C], F32, name="shared1", tag="dy1", align_bytes=64)
-        factor1 = shared1[:, 0, early:].rearrange("p (h d s) -> p h d s", h=2, d=PACK)
-        picked = shared1[:, 1, early:].rearrange("p (d s) -> p d s", d=PACK)
+        window = [held.tile([P, T], F32, name=f"window{b}") for b in range(BLOCKS)]
+        codes = [held.tile([P, C], I32, name=f"codes{e}", align_bytes=64) for e in range(E)]
+        plane = [held.tile([P, C], U8, name=f"plane{e}", align_bytes=64) for e in range(E)]
+        da0 = held.tile([P, PACK, C], F32, name="da0")
+        picked = held.tile([P, PACK, C], F32, name="picked", tag="dy1", align_bytes=64)
         halves = [slice(0, GROUP), slice(GROUP, C)]
 
         def result(g, b):
-            if g == 1:
-                return banks[4 + b // 2][:, halves[b % 2]]
-            return banks[((1, 2, 3), (), (7, 6, 1), (2, 3, 4))[g][(1, 2, 0, 0)[b]]][:, halves[b // 3]]
+            bank, half = (
+                ((1, 0), (2, 1), (3, 0), (6, 1)),
+                ((2, 0), (4, 0), (5, 0), (5, 1)),
+                ((6, 0), (7, 0), (3, 0), (3, 1)),
+                ((1, 0), (2, 0), (0, 0), (0, 1)),
+            )[g][b]
+            return banks[bank][:, halves[half]]
 
         def quantize_and_multiply(g, woven):
-            nc.vector.quantize_mx(out=codes[:].bitcast(E5M2), scales=plane[:], in_=woven[:])
+            e, cols = g // 2, halves[g % 2]
+            nc.vector.quantize_mx(out=codes[e][:, cols].bitcast(E5M2), scales=plane[e][:, cols], in_=woven[:])
             for b in (2, 3, 0, 1):
                 rows = slice(b * P, (b + 1) * P)
                 nc.tensor.matmul_mx(
-                    out=result(g, b), lhsT=w1_codes[:, g // 2, rows].bitcast(E4M3), lhsT_scale=w1_plane[:, g // 2, rows],
-                    rhs=codes[:].bitcast(E5M2), rhs_scale=plane[:], start=True, stop=True,
+                    out=result(g, b), lhsT=w1_codes[:, e, rows].bitcast(E4M3), lhsT_scale=w1_plane[:, e, rows],
+                    rhs=codes[e][:, cols].bitcast(E5M2), rhs_scale=plane[e][:, cols], start=True, stop=True,
                 )
 
         def vector_scatter(b, first, count, src):
             nc.vector.tensor_copy(window[b][:].indirect(slots(first, count)), src)
 
-        def vector_copies(g, staged):
-            for b in range(2):
-                nc.vector.tensor_copy(out=staged[b], in_=result(g, b))
+        def vector_copy(g, b, staged):
+            nc.vector.tensor_copy(out=staged, in_=result(g, b))
 
         def scalar_group(g):
             dx = held.tile([P, C], F32, name=f"dx_scalar{g}")
@@ -170,79 +168,83 @@ def tile_moe_sdb_relu_kernel(
         def woven_tile(g):
             return held.tile([P, GROUP * PACK], BF16, name=f"woven{g}", tag="woven", align_bytes=64)
 
-        def weave0(h):
-            woven = woven_tile(h)
-            nc.gpsimd.tensor_scalar(
-                woven[:].rearrange("p (s d) -> p s d", d=PACK), da0[:, :, halves[h]].rearrange("p d s -> p s d"),
-                1.0, 0.0, ALU.mult, ALU.add,
-            )
-            return woven
-
         def weave1(h):
             woven = woven_tile(2 + h)
             nc.gpsimd.tensor_tensor(
-                woven_by_two(woven[:]), strands_by_two(picked[:, :, halves[h]]), strands_by_two(factor1[:, h]),
-                ALU.mult,
+                woven_by_two(woven[:]), strands_by_two(picked[:, :, halves[h]]), strands_by_two(factor1[h]), ALU.mult
             )
             return woven
-
-        def factor(dst, saved, gate_rows):
-            nc.vector.scalar_tensor_tensor(out=dst, in0=saved, scalar=0.0, in1=gate_rows, op0=ALU.is_gt, op1=ALU.mult)
 
         def by_fours(ap):
             return ap.rearrange("p (n c) -> p n c", c=PACK)
 
-        def by_halves(ap):
-            return ap.rearrange("p (h s) -> p h s", h=2)
-
         last = PACK - 1
         factor0 = [held.tile([P, C], F32, name=f"factor0{d}") for d in range(PACK)]
+        shared = held.tile([P, GROUP + PACK * C], F32, name="shared")
+        factor1 = [
+            shared[:, (1 + PACK * h) * GROUP : (1 + PACK * (h + 1)) * GROUP].rearrange("p (d s) -> p d s", d=PACK)
+            for h in range(2)
+        ]
 
-        factor(by_fours(factor0[0][:]), by_fours(a0[0][:]), gate0)
+        def factor0_strand(d):
+            nc.vector.scalar_tensor_tensor(
+                out=by_fours(factor0[d][:]), in0=by_fours(a0[d][:]), scalar=0.0, in1=gate0, op0=ALU.is_gt, op1=ALU.mult
+            )
+
+        def factor1_strands(h, first, count):
+            strands = slice(first, first + count)
+            nc.vector.scalar_tensor_tensor(
+                out=factor1[h][:, strands, :], in0=a1[:, strands, halves[h]], scalar=0.0,
+                in1=gate1[:, halves[h]].unsqueeze(1).to_broadcast([P, count, GROUP]), op0=ALU.is_gt, op1=ALU.mult,
+            )
+
+        factor0_strand(0)
         for d in range(last):
-            factor(by_fours(factor0[d + 1][:]), by_fours(a0[d + 1][:]), gate0)
+            factor0_strand(d + 1)
             nc.vector.tensor_tensor(da0[:, d, :], dc[d][:].indirect(slots(0, C)), factor0[d][:], ALU.mult)
         for d in range(PACK):
             nc.scalar.activation(picked[:, d, :], dc[d][:].indirect(slots(C, C)), ACT.Copy)
-
-        def last_gather(h):
+        for h in range(2):
             nc.vector.tensor_tensor(
                 da0[:, last, halves[h]], dc[last][:].indirect(slots(h * GROUP, GROUP)), factor0[last][:, halves[h]], ALU.mult
             )
-
-        last_gather(0)
-        woven = weave0(0)
-        for d in range(last):
-            factor(factor1[:, :, d, :], by_halves(a1[:, d, :]), by_halves(gate1[:]))
+        woven = woven_tile(0)
+        nc.vector.tensor_copy(out=woven_by_two(woven[:]), in_=strands_by_two(da0[:, :, halves[0]]))
+        factor1_strands(0, 0, 2)
         quantize_and_multiply(0, woven)
-        last_gather(1)
-        woven = weave0(1)
-        factor(factor1[:, :, last, :], by_halves(a1[:, last, :]), by_halves(gate1[:]))
+        woven = woven_tile(1)
+        nc.gpsimd.tensor_scalar(
+            woven[:].rearrange("p (s d) -> p s d", d=PACK), da0[:, :, halves[1]].rearrange("p d s -> p s d"),
+            1.0, 0.0, ALU.mult, ALU.add,
+        )
+        factor1_strands(0, 2, 2)
+        factor1_strands(1, 0, PACK)
         scalar_group(0)
-        dx_a = held.tile([P, 2, GROUP], F32, name="dx_a")
-        vector_copies(0, [dx_a[:, b, :] for b in range(2)])
+        dx0 = held.tile([P, C], F32, name="dx0")
+        dx1 = [shared[:, 0:C], held.tile([P, C], F32, name="dx1")[:]]
+        vector_copy(0, 0, dx0[:, halves[0]])
         quantize_and_multiply(1, woven)
         woven = weave1(0)
-        for b in range(2):
-            window[b] = placed.tile([P, T], F32, name=f"window{b}", offset=4 * T * b)
-            vector_scatter(b, 0, GROUP, dx_a[:, b, :])
+        vector_scatter(0, 0, GROUP, dx0[:, halves[0]])
         scalar_group(1)
-        for cols in (slice(0, early), slice(early, GROUP)):
-            nc.vector.tensor_copy(out=shared1[:, :, cols], in_=by_halves(banks[4][:])[:, :, cols])
+        vector_copy(1, 0, dx0[:, halves[1]])
+        vector_copy(0, 1, dx1[0][:, halves[0]])
+        vector_scatter(0, GROUP, GROUP, dx0[:, halves[1]])
+        vector_copy(1, 1, dx1[0][:, halves[1]])
         quantize_and_multiply(2, woven)
         woven = weave1(1)
-        for b in range(2):
-            vector_scatter(b, GROUP, GROUP, shared1[:, b, 0:GROUP])
+        vector_scatter(1, 0, C, dx1[0])
         scalar_group(2)
-        dx1 = held.tile([P, C], F32, name="dx1")
-        dx_c = factor1[:, 1, 0, :]
+        dx_c = picked[:, 0, halves[1]]
         dx_d = held.tile([P, GROUP], F32, name="dx_d")
-        vector_copies(2, [dx_c, dx1[:, halves[0]]])
+        vector_copy(2, 0, dx_c)
+        vector_copy(2, 1, dx1[1][:, halves[0]])
         quantize_and_multiply(3, woven)
         vector_scatter(0, C, GROUP, dx_c)
         scalar_group(3)
-        vector_copies(3, [dx_d[:], dx1[:, halves[1]]])
+        vector_copy(3, 0, dx_d[:])
+        vector_copy(3, 1, dx1[1][:, halves[1]])
         vector_scatter(0, C + GROUP, GROUP, dx_d[:])
-        vector_scatter(1, C, C, dx1[:])
+        vector_scatter(1, C, C, dx1[1])
         for b in (0, 2, 3, 1):
             nc.sync.dma_start(out=out[b * P : (b + 1) * P, :], in_=window[b][:])

@@ -83,12 +83,13 @@ def tile_moe_sdb_relu_kernel(
         nc.sync.dma_start(out=a1[:], in_=a_rows[:, :, C : 2 * C])
 
         make_identity(nc, identity[:])
-        gate_bank = banks[BANKS - 1]
-        for c in range(PACK):
-            nc.tensor.transpose(
-                gate_bank[:, c * P : (c + 1) * P], gate_cols[:, c : c + 1].to_broadcast([P, P]), identity[:]
-            )
-        gate0 = gate_bank[:].rearrange("p (c n) -> p n c", c=PACK)
+
+        def spread_gate(cols, bank):
+            for c in range(PACK):
+                nc.tensor.transpose(bank[:, c * P : (c + 1) * P], cols[:, c : c + 1].to_broadcast([P, P]), identity[:])
+            return bank[:].rearrange("p (c n) -> p n c", c=PACK)
+
+        gate0 = spread_gate(gate_cols, banks[BANKS - 1])
 
         for q in range(4):
             nc.vector.tensor_copy(out=w2_zeroed[32 * q : 32 * q + 4, :].bitcast(I32), in_=w2_rows[64 * (q // 2) : 64 * (q // 2) + 4, q % 2, :].bitcast(I32))
@@ -119,9 +120,7 @@ def tile_moe_sdb_relu_kernel(
                 )
                 nc.scalar.copy(out=dc[d][:, toks], in_=bank[:])
 
-        gate1 = banks[0]
-        for c in range(PACK):
-            nc.tensor.transpose(gate1[:, c:C:PACK], gate1_cols[:, c : c + 1].to_broadcast([P, P]), identity[:])
+        gate1 = spread_gate(gate1_cols, banks[3])
 
         def slots(first, count):
             return offsets[:, first // 16 : (first + count) // 16]
@@ -135,10 +134,10 @@ def tile_moe_sdb_relu_kernel(
 
         def result(g, b):
             bank, half = (
-                ((1, 0), (2, 1), (3, 0), (6, 1)),
-                ((2, 0), (4, 0), (5, 0), (5, 1)),
-                ((6, 0), (7, 0), (3, 0), (3, 1)),
-                ((1, 0), (2, 0), (0, 0), (0, 1)),
+                ((1, 0), (2, 1), (4, 0), (6, 1)),
+                ((2, 0), (0, 0), (5, 0), (5, 1)),
+                ((6, 0), (7, 0), (4, 0), (4, 1)),
+                ((1, 0), (2, 0), (3, 0), (3, 1)),
             )[g][b]
             return banks[bank][:, halves[half]]
 
@@ -171,7 +170,7 @@ def tile_moe_sdb_relu_kernel(
         def weave1(h):
             woven = woven_tile(2 + h)
             nc.gpsimd.tensor_tensor(
-                woven_by_two(woven[:]), strands_by_two(picked[:, :, halves[h]]), strands_by_two(factor1[h]), ALU.mult
+                woven_by_two(woven[:]), strands_by_two(picked[:, :, halves[h]]), strands_by_two(factor1[:, :, halves[h]]), ALU.mult
             )
             return woven
 
@@ -179,24 +178,15 @@ def tile_moe_sdb_relu_kernel(
             return ap.rearrange("p (n c) -> p n c", c=PACK)
 
         last = PACK - 1
-        factor0 = [held.tile([P, C], F32, name=f"factor0{d}") for d in range(PACK)]
-        shared = held.tile([P, GROUP + PACK * C], F32, name="shared")
-        factor1 = [
-            shared[:, (1 + PACK * h) * GROUP : (1 + PACK * (h + 1)) * GROUP].rearrange("p (d s) -> p d s", d=PACK)
-            for h in range(2)
-        ]
+        factor0 = [held.tile([P, C], F32, name=f"factor0{d}", tag=f"factor{d}") for d in range(PACK)]
+
+        def factor(dst, saved, gate_rows):
+            nc.vector.scalar_tensor_tensor(
+                out=by_fours(dst), in0=by_fours(saved), scalar=0.0, in1=gate_rows, op0=ALU.is_gt, op1=ALU.mult
+            )
 
         def factor0_strand(d):
-            nc.vector.scalar_tensor_tensor(
-                out=by_fours(factor0[d][:]), in0=by_fours(a0[d][:]), scalar=0.0, in1=gate0, op0=ALU.is_gt, op1=ALU.mult
-            )
-
-        def factor1_strands(h, first, count):
-            strands = slice(first, first + count)
-            nc.vector.scalar_tensor_tensor(
-                out=factor1[h][:, strands, :], in0=a1[:, strands, halves[h]], scalar=0.0,
-                in1=gate1[:, halves[h]].unsqueeze(1).to_broadcast([P, count, GROUP]), op0=ALU.is_gt, op1=ALU.mult,
-            )
+            factor(factor0[d][:], a0[d][:], gate0)
 
         factor0_strand(0)
         for d in range(last):
@@ -210,15 +200,17 @@ def tile_moe_sdb_relu_kernel(
             )
         woven = woven_tile(0)
         nc.vector.tensor_copy(out=woven_by_two(woven[:]), in_=strands_by_two(da0[:, :, halves[0]]))
-        factor1_strands(0, 0, 2)
+        shared = held.tile([P, GROUP + PACK * C], F32, name="shared", tag=f"factor{last}")
+        factor1 = shared[:, GROUP:].rearrange("p (d s) -> p d s", d=PACK)
+        factor(factor1[:, 0, :], a1[:, 0, :], gate1)
         quantize_and_multiply(0, woven)
         woven = woven_tile(1)
         nc.gpsimd.tensor_scalar(
             woven[:].rearrange("p (s d) -> p s d", d=PACK), da0[:, :, halves[1]].rearrange("p d s -> p s d"),
             1.0, 0.0, ALU.mult, ALU.add,
         )
-        factor1_strands(0, 2, 2)
-        factor1_strands(1, 0, PACK)
+        for d in range(1, PACK):
+            factor(factor1[:, d, :], a1[:, d, :], gate1)
         scalar_group(0)
         dx0 = held.tile([P, C], F32, name="dx0")
         dx1 = [shared[:, 0:C], held.tile([P, C], F32, name="dx1")[:]]

from contextlib import ExitStack

import concourse.mybir as mybir
from concourse.masks import make_identity

K, T, E, C, H, N = 512, 1024, 2, 512, 512, 512
P = 128
PACK = 4
GROUP = 256
BLOCKS = K // P
BANKS = 8
FLOPS = 2 * N * H * T + 2 * H * K * E * C

F32 = mybir.dt.float32
BF16 = mybir.dt.bfloat16
I32 = mybir.dt.int32
U16 = mybir.dt.uint16
U8 = mybir.dt.uint8
E4M3 = mybir.dt.float8_e4m3fn_x4
E5M2 = mybir.dt.float8_e5m2_x4
ALU = mybir.AluOpType
ACT = mybir.ActivationFunctionType


def strands_by_two(ap):
    return ap.rearrange("p d (c i) -> p c d i", i=2)


def woven_by_two(ap):
    return ap.rearrange("p (c i d) -> p c d i", i=2, d=PACK)


def tile_moe_sdb_relu_kernel(
    tc, dy_words, dy_scales, w2t_words, w2t_scales, w1t_words, w1t_scales, a, gate, offs, out
):
    nc = tc.nc
    with ExitStack() as ctx:
        held = ctx.enter_context(tc.tile_pool(name="held", bufs=1))
        psum = ctx.enter_context(tc.psum_pool(name="psum", bufs=1))

        offsets = held.tile([P, E * C // 16], U16, name="offsets")
        w2_raw = held.tile([P, H], I32, name="w2_raw", align_bytes=64)
        w2_rows = held.tile([P, 2, H], U8, name="w2_rows", align_bytes=64)
        w2_zeroed = held.tile([P, H], U8, name="w2_zeroed", align_bytes=64)
        dy_codes = [held.tile([P, C], I32, name=f"dy_codes{h}", tag=f"dy{h}", align_bytes=64) for h in range(2)]
        dy_rows = held.tile([P, 2, T], U8, name="dy_rows", align_bytes=64)
        dy_plane = dy_rows[:, 0, :]
        w1_codes = held.tile([P, E, K], I32, name="w1_codes", align_bytes=64)
        w1_plane = held.tile([P, E, K], U8, name="w1_plane", align_bytes=64)
        gate_cols = held.tile([P, PACK], F32, name="gate_cols", tag="gate_cols", align_bytes=64)
        gate1_cols = held.tile([P, PACK], F32, name="gate1_cols")
        identity = held.tile([P, P], F32, name="identity")
        banks = [psum.tile([P, C], F32, name=f"bank{b}") for b in range(BANKS)]
        a0 = [held.tile([P, C], F32, name=f"a0{d}") for d in range(PACK)]
        a1 = held.tile([P, PACK, C], F32, name="a1")

        nc.vector.memset(w2_zeroed[:].bitcast(I32), 0)

        a_rows = a.rearrange("(p d) s -> p d s", d=PACK)
        for rows, scales in ((w2_rows, w2t_scales), (dy_rows, dy_scales)):
            for u in range(2):
                nc.sync.dma_start(
                    out=rows[64 * u : 64 * u + 4].bitcast(I32),
                    in_=scales[0, 8 * u : 8 * u + 8].rearrange("(q r) i -> r q i", r=4).bitcast(I32),
                )
            if rows is w2_rows:
                nc.sync.dma_start(out=gate_cols[:], in_=gate[0, 0:C].rearrange("(p c) -> p c", c=PACK))
        nc.sync.dma_start(out=w2_raw[:], in_=w2t_words[0].rearrange("p i d -> p (i d)").bitcast(I32))
        dy_flat = dy_words[0].rearrange("p t d -> p (t d)").bitcast(I32)
        for h in range(2):
            nc.sync.dma_start(out=dy_codes[h][:], in_=dy_flat[:, h * C : (h + 1) * C])
        for d in range(PACK):
            nc.sync.dma_start(out=a0[d][:], in_=a_rows[:, d, 0:C])
            if d == 1:
                nc.sync.dma_start(offsets[:], offs)
        nc.sync.dma_start(out=gate1_cols[:], in_=gate[0, C : 2 * C].rearrange("(p c) -> p c", c=PACK))
        nc.sync.dma_start(out=w1_codes[:], in_=w1t_words[:, 0].rearrange("e p k d -> p e (k d)").bitcast(I32))
        for r in range(4):
            nc.sync.dma_start(
                out=w1_plane[r:P:32, :, :].bitcast(I32),
                in_=w1t_scales[:, 0, r:16:4, :].rearrange("e q k -> q e k").bitcast(I32),
            )
        nc.sync.dma_start(out=a1[:], in_=a_rows[:, :, C : 2 * C])

        make_identity(nc, identity[:])

        def spread_gate(cols, bank):
            for c in range(PACK):
                nc.tensor.transpose(bank[:, c * P : (c + 1) * P], cols[:, c : c + 1].to_broadcast([P, P]), identity[:])
            return bank[:].rearrange("p (c n) -> p n c", c=PACK)

        gate0 = spread_gate(gate_cols, banks[BANKS - 1])

        for q in range(4):
            nc.vector.tensor_copy(out=w2_zeroed[32 * q : 32 * q + 4, :].bitcast(I32), in_=w2_rows[64 * (q // 2) : 64 * (q // 2) + 4, q % 2, :].bitcast(I32))
        w2_codes = held.tile([P, H], I32, name="w2_codes", tag="gate_cols", align_bytes=64)
        w2_plane = held.tile([P, H], U8, name="w2_plane", align_bytes=64)
        nc.vector.tensor_copy(
            out=w2_plane[:].rearrange("p (d c i) -> p c d i", d=PACK, i=16),
            in_=w2_zeroed[:].rearrange("p (c i d) -> p c d i", d=PACK, i=16),
        )
        for u in range(2):
            nc.vector.tensor_copy(
                out=dy_plane[64 * u + 32 : 64 * u + 36, :].bitcast(I32), in_=dy_rows[64 * u : 64 * u + 4, 1, :].bitcast(I32)
            )
        nc.vector.tensor_copy(
            out=w2_codes[:].rearrange("p (d c i) -> p c d i", d=PACK, i=4),
            in_=w2_raw[:].rearrange("p (c i d) -> p c d i", d=PACK, i=4),
        )

        dc = [held.tile([P, T], F32, name=f"dc{d}") for d in range(PACK)]
        for d in range(PACK):
            cols = slice(d * P, (d + 1) * P)
            for h in range(2):
                toks = slice(h * C, (h + 1) * C)
                bank = banks[(2 * d + h) % (BANKS - 1)]
                nc.tensor.matmul_mx(
                    out=bank[:], lhsT=w2_codes[:, cols].bitcast(E4M3), lhsT_scale=w2_plane[:, cols],
                    rhs=dy_codes[h][:].bitcast(E5M2), rhs_scale=dy_plane[:, toks], start=True, stop=True,
                )
                nc.scalar.copy(out=dc[d][:, toks], in_=bank[:])

        gate1 = spread_gate(gate1_cols, banks[3])

        def slots(first, count):
            return offsets[:, first // 16 : (first + count) // 16]

        window = [held.tile([P, T], F32, name=f"window{b}") for b in range(BLOCKS)]
        codes = [held.tile([P, C], I32, name=f"codes{e}", align_bytes=64) for e in range(E)]
        plane = [held.tile([P, C], U8, name=f"plane{e}", align_bytes=64) for e in range(E)]
        da0 = held.tile([P, PACK, C], F32, name="da0")
        picked = held.tile([P, PACK, C], F32, name="picked", tag="dy1", align_bytes=64)
        halves = [slice(0, GROUP), slice(GROUP, C)]

        def result(g, b):
            bank, half = (
                ((1, 0), (2, 1), (4, 0), (6, 1)),
                ((2, 0), (0, 0), (5, 0), (5, 1)),
                ((6, 0), (7, 0), (4, 0), (4, 1)),
                ((1, 0), (2, 0), (3, 0), (3, 1)),
            )[g][b]
            return banks[bank][:, halves[half]]

        def quantize_and_multiply(g, woven):
            e, cols = g // 2, halves[g % 2]
            nc.vector.quantize_mx(out=codes[e][:, cols].bitcast(E5M2), scales=plane[e][:, cols], in_=woven[:])
            for b in (2, 3, 0, 1):
                rows = slice(b * P, (b + 1) * P)
                nc.tensor.matmul_mx(
                    out=result(g, b), lhsT=w1_codes[:, e, rows].bitcast(E4M3), lhsT_scale=w1_plane[:, e, rows],
                    rhs=codes[e][:, cols].bitcast(E5M2), rhs_scale=plane[e][:, cols], start=True, stop=True,
                )

        def vector_scatter(b, first, count, src):
            nc.vector.tensor_copy(window[b][:].indirect(slots(first, count)), src)

        def vector_copy(g, b, staged):
            nc.vector.tensor_copy(out=staged, in_=result(g, b))

        def scalar_group(g):
            dx = held.tile([P, C], F32, name=f"dx_scalar{g}")
            for b in range(2):
                nc.scalar.copy(out=dx[:, halves[b]], in_=result(g, 2 + b))
            for b in range(2):
                nc.scalar.activation(window[2 + b][:].indirect(slots(g * GROUP, GROUP)), dx[:, halves[b]], ACT.Copy)

        def woven_tile(g):
            return held.tile([P, GROUP * PACK], BF16, name=f"woven{g}", tag="woven", align_bytes=64)

        def weave1(h):
            woven = woven_tile(2 + h)
            nc.gpsimd.tensor_tensor(
                woven_by_two(woven[:]), strands_by_two(picked[:, :, halves[h]]), strands_by_two(factor1[:, :, halves[h]]), ALU.mult
            )
            return woven

        def by_fours(ap):
            return ap.rearrange("p (n c) -> p n c", c=PACK)

        last = PACK - 1
        factor0 = [held.tile([P, C], F32, name=f"factor0{d}", tag=f"factor{d}") for d in range(PACK)]

        def factor(dst, saved, gate_rows):
            nc.vector.scalar_tensor_tensor(
                out=by_fours(dst), in0=by_fours(saved), scalar=0.0, in1=gate_rows, op0=ALU.is_gt, op1=ALU.mult
            )

        def factor0_strand(d):
            factor(factor0[d][:], a0[d][:], gate0)

        factor0_strand(0)
        for d in range(last):
            factor0_strand(d + 1)
            nc.vector.tensor_tensor(da0[:, d, :], dc[d][:].indirect(slots(0, C)), factor0[d][:], ALU.mult)
        for d in range(PACK):
            nc.scalar.activation(picked[:, d, :], dc[d][:].indirect(slots(C, C)), ACT.Copy)
        for h in range(2):
            nc.vector.tensor_tensor(
                da0[:, last, halves[h]], dc[last][:].indirect(slots(h * GROUP, GROUP)), factor0[last][:, halves[h]], ALU.mult
            )
        woven = woven_tile(0)
        nc.vector.tensor_copy(out=woven_by_two(woven[:]), in_=strands_by_two(da0[:, :, halves[0]]))
        shared = held.tile([P, GROUP + PACK * C], F32, name="shared", tag=f"factor{last}")
        factor1 = shared[:, GROUP:].rearrange("p (d s) -> p d s", d=PACK)
        factor(factor1[:, 0, :], a1[:, 0, :], gate1)
        quantize_and_multiply(0, woven)
        woven = woven_tile(1)
        nc.gpsimd.tensor_scalar(
            woven[:].rearrange("p (s d) -> p s d", d=PACK), da0[:, :, halves[1]].rearrange("p d s -> p s d"),
            1.0, 0.0, ALU.mult, ALU.add,
        )
        for d in range(1, PACK):
            factor(factor1[:, d, :], a1[:, d, :], gate1)
        scalar_group(0)
        dx0 = held.tile([P, C], F32, name="dx0")
        dx1 = [shared[:, 0:C], held.tile([P, C], F32, name="dx1")[:]]
        vector_copy(0, 0, dx0[:, halves[0]])
        quantize_and_multiply(1, woven)
        woven = weave1(0)
        vector_scatter(0, 0, GROUP, dx0[:, halves[0]])
        scalar_group(1)
        vector_copy(1, 0, dx0[:, halves[1]])
        vector_copy(0, 1, dx1[0][:, halves[0]])
        vector_scatter(0, GROUP, GROUP, dx0[:, halves[1]])
        vector_copy(1, 1, dx1[0][:, halves[1]])
        quantize_and_multiply(2, woven)
        woven = weave1(1)
        vector_scatter(1, 0, C, dx1[0])
        scalar_group(2)
        dx_c = picked[:, 0, halves[1]]
        dx_d = held.tile([P, GROUP], F32, name="dx_d")
        vector_copy(2, 0, dx_c)
        vector_copy(2, 1, dx1[1][:, halves[0]])
        quantize_and_multiply(3, woven)
        vector_scatter(0, C, GROUP, dx_c)
        scalar_group(3)
        vector_copy(3, 0, dx_d[:])
        vector_copy(3, 1, dx1[1][:, halves[1]])
        vector_scatter(0, C + GROUP, GROUP, dx_d[:])
        vector_scatter(1, C, C, dx1[1])
        for b in (0, 2, 3, 1):
            nc.sync.dma_start(out=out[b * P : (b + 1) * P, :], in_=window[b][:])
